import numpy as np, ml_dtypes
CORES = [2,3,42,43,82,83,122,123]
N = 8
BF = ml_dtypes.bfloat16
W, A, S, RO, H = 4096, 128, 2, 8, 2
def parts(rng):
    z = rng.integers(0, 256, (N, 8, 16, W)); w = rng.integers(0, 256, (N, 8, 16, 3)); w[..., 2] = rng.integers(0, 2048, (N, 8, 16))
    return z, w, rng.choice(np.array([750, 850, 950, 1200]), (N, 8, 1, 1))
def loose(rng):
    share = rng.choice(np.array([0.06, 0.15, 0.4, 0.9]), (N, 8, 1, A))
    return np.where(rng.random((N, 8, 16, A)) < share, rng.integers(0, W, (N, 8, 16, A)), -1)
def objects(rng, z, n):
    ix = np.argsort(rng.random((N, 8, W)), axis=-1)[..., :S * 2 * n]
    base = rng.integers(40, 216, (8, 16, 1, 1, n)); dev = rng.integers(-16, 17, (8, 16, 16, 2, n))
    order = np.argsort(rng.random((8, 16, n)), axis=1); rows = np.arange(16)[None, :, None]
    up = rows == order[:, :1]; down = rows == order[:, 1:2]
    v = base + np.where(up[:, None, :, None, :], 16, np.where(down[:, None, :, None, :], -16, dev))
    for q in range(N):
        np.put_along_axis(z[q], np.broadcast_to(ix[q][:, None, :], (8, 16, S * 2 * n)), v[:, :, S * q:S * q + S].reshape(8, 16, S * 2 * n), 2)
    return np.ascontiguousarray(ix.reshape(N, 8, S, 2, n).transpose(1, 0, 2, 3, 4)).reshape(8, 16, 2, n), up | down
def follow(rng, obj, am):
    out = []
    for r in range(N):
        c = rng.integers(0, obj.shape[-1], (8, 1, A))
        one = np.take_along_axis(obj[:, :, 0], c, 2); two = np.take_along_axis(obj[:, :, 1], c, 2); anchor = np.take_along_axis(am, c, 2)
        v = (rng.random((8, 16, A)) < rng.choice(np.array([0, 0, 0.1, 0.5]), (8, 1, A))) & ~anchor
        keep = anchor | (rng.random((8, 16, A)) < rng.random((8, 1, A)))
        out.append(np.where(keep, np.where(v, two, one), -1))
    return np.stack(out)
def pack(z, w, t, p, s):
    return {"tz": np.ascontiguousarray(z.reshape(N, 128, W)).astype(np.float32).astype(BF), "tp": np.ascontiguousarray(p.reshape(N, 128, A)).astype(np.int32),
            "sd": np.ascontiguousarray(s.reshape(N, 128, A)).astype(np.int32), "hw": np.ascontiguousarray(w.reshape(N, 128, 3)).astype(np.int32),
            "th": np.repeat(t.reshape(N, 8, 1), 16, axis=1).astype(np.int32)}
def setup_inputs(rng):
    z, w, t = parts(rng); obj, am = objects(rng, z, A // 4)
    p = np.where(rng.random((N, 8, 1, A)) < 0.5, follow(rng, obj, am), loose(rng))
    s = np.where(rng.random((N, 8, 1, A)) < 0.5, follow(rng, obj, am), loose(rng))
    return pack(z, w, t, p, s)
def setup_inputs_twins(rng):
    z, w, t = parts(rng); obj, am = objects(rng, z, 4); t[:] = 4096
    p = follow(rng, obj, am); p[:, 6:] = loose(rng)[:, 6:]; p[..., A // 2:] = p[..., :A // 2].copy()
    return pack(z, w, t, p, follow(rng, obj, am))
def setup_inputs_ties(rng):
    z, w, t = parts(rng)
    z = np.take_along_axis(rng.integers(0, 256, (N, 8, 16, 6)), rng.integers(0, 6, (N, 8, 1, W)), 3)
    t = rng.choice(np.array([1000, 4096]), (N, 8, 1, 1)); p = loose(rng); s = loose(rng)
    w[:, 0, :, :2] = 0; w[:, 1, :, 2] = 0; w[:, 4, :, 2] = rng.choice(np.array([5, 1031]), (N, 16)); t[:, :2] = 4096
    z[:, 2:4] = 100; t[::2, 2] = 0; t[1::2, 2] = 1; t[:, 3] = 432; p[:, 2:4, :, ::4] = -1
    return pack(z, w, t, p, s)
def setup_inputs_ends(rng):
    z = 255 * rng.integers(0, 2, (N, 8, 16, W)); ends = np.array([-1, 0, 1, W - 2, W - 1])
    p = rng.choice(ends, (N, 8, 16, A)); s = rng.choice(ends, (N, 8, 16, A)); t = rng.choice(np.array([0, 1, 2040, 4080, 4096]), (N, 8, 1, 1))
    w = rng.choice(np.array([0, 1, 254, 255]), (N, 8, 16, 3)); w[..., 2] = rng.choice(np.array([0, 1, 1025, 2046, 2047]), (N, 8, 16))
    p[:, 4] = rng.integers(0, W, (N, 16, A)); t[:, 4] = 4096
    z[:, 5] = 255; w[:, 5, :, :2] = 0; w[:, 5, 0, :2] = 255; w[:, 5, 1, :2] = 2; w[:, 5, :, 2] = 2047; t[:, 5] = 4096
    p[:, 6] = -1; t[:, 6] = 4096
    z[::2, 7] = 255; z[1::2, 7] = 0; p[:, 7] = rng.integers(0, W, (N, 16, A)); p[:, 7, (np.arange(16) // S) % 2 == 1] = -1
    t[1::4, 7] = 4081; t[3::4, 7] = 4080
    w[1::2, 7, :, 0] = 0; w[1::2, 7, :, 1] = 254 * rng.integers(0, 2, (N // 2, 16)); w[1::2, 7, 0, 1] = 255; w[1::2, 7, 0, 2] = rng.integers(1, 2048, N // 2)
    return pack(z, w, t, p, s)
def setup_inputs_sparse(rng):
    z, w, t = parts(rng); t = rng.choice(np.array([900, 4096]), (N, 8, 1, 1)); t[:, 0] = 4096
    p = np.where(rng.random((N, 8, 16, A)) < 0.06, rng.integers(0, W, (N, 8, 16, A)), -1); p[rng.integers(0, N)] = -1
    s = loose(rng); s[:, rng.permutation(8)[:4]] = -1
    return pack(z, w, t, p, s)
def setup_inputs_spread(rng):
    z = np.minimum((np.exp2(8.0 * rng.random((N, 8, 1, W))) * rng.random((N, 8, 16, W))).astype(np.int64), 255)
    w = np.minimum(np.exp2(8.0 * rng.random((N, 8, 16, 3))).astype(np.int64), 255); w[..., 2] = np.minimum(np.exp2(11.0 * rng.random((N, 8, 16))).astype(np.int64), 2047)
    t = np.minimum(np.exp2(7.0 + 5.0 * rng.random((N, 8, 1, 1))).astype(np.int64), 4096)
    ps = []
    for i in range(2):
        nm = np.minimum((W * rng.random((N, 8, 16, A)) ** 3).astype(np.int64), W - 1)
        ps.append(np.where(rng.random((N, 8, 16, A)) < rng.random((N, 8, 1, A)), nm, -1))
    return pack(z, w, t, ps[0], ps[1])
def check_inputs(d):
    bad = []; v = np.asarray(d["tz"]).astype(np.float32)
    if not (np.min(v) >= 0 and np.max(v) <= 255 and np.all(v == np.floor(v))): bad.append("tz: whole numbers from 0 to 255")
    for k, lo, hi in (("tp", -1, W - 1), ("sd", -1, W - 1), ("th", 0, 4096)):
        if np.min(d[k]) < lo or np.max(d[k]) > hi: bad.append("range of " + k)
    w = np.asarray(d["hw"])
    if np.min(w) < 0 or np.max(w[..., :2]) > 255 or np.max(w[..., 2]) > 2047: bad.append("range of hw")
    t = np.asarray(d["th"]).reshape(-1, 16)
    if np.any(t != t[:, :1]): bad.append("th: one number a group")
    return bad
def reference(tz, tp, sd, hw, th):
    z = tz.astype(np.float32).astype(np.int32).reshape(N, 8, 16, W); w = hw.astype(np.int32).reshape(N, 8, 16, 3); lim = th.astype(np.int32).reshape(N, 8, 16)[:, :, :1]
    p = tp.astype(np.int32).reshape(N, 8, 16, A); s = sd.astype(np.int32).reshape(N, 8, 16, A); lower = np.arange(A)[None, :] < np.arange(A)[:, None]
    for t in range(RO):
        for r in range(N):
            q = (r + 1 + t) % N; x = S * q + t // N
            hi = np.zeros((8, 16, A), np.int32); lo = np.full((8, 16, A), 255, np.int32)
            for j in range(16):
                n = p[r, :, j]; on = (n >= 0)[:, None, :]; v = np.take_along_axis(z[j // S], np.maximum(n, 0)[:, None, :], 2)
                hi = np.where(on, np.maximum(hi, v), hi); lo = np.where(on, np.minimum(lo, v), lo)
            e = (hi + lo) >> 1; c = e
            best = np.full((8, A), 4097); name = np.zeros((8, A), np.int64)
            for k in range(H):
                u1 = np.add.reduce(w[q, :, :, 0:1] * c, axis=1) & (W - 1); u2 = np.add.reduce(w[q, :, :, 1:2] * c, axis=1) & (W - 1)
                h = (((u1 * u2) >> 5)[:, None, :] + w[q, :, :, 2:3] * u2[:, None, :]) & (W - 1)
                v = np.take_along_axis(z[q], h.reshape(8, 1, 16 * A), 2).reshape(8, 16, 16, A)
                d = np.add.reduce(np.abs(v - e[:, :, None, :]), axis=1)
                m = np.argmin(d, axis=1); dm = np.min(d, axis=1); n = np.take_along_axis(h, m[:, None, :], 1)[:, 0]
                less = dm < best; name = np.where(less, n, name); best = np.where(less, dm, best)
                c = (e + np.take_along_axis(z[q], n[:, None, :], 2)) >> 1
            n = np.where(best < lim[q], name, -1); p[r, :, x] = n
            low = (n[:, :, None] == n[:, None, :]) & (n >= 0)[:, :, None] & lower
            g, b = np.nonzero(np.count_nonzero(low, axis=2) == 1); a = np.argmax(low[g, b], axis=1)
            pa = p[r][g, :, a]; pb = p[r][g, :, b]; differ = (pa >= 0) & (pb >= 0) & (pa != pb); clash = np.any(differ, axis=1)[:, None]
            p[r][g, :, a] = np.where(clash, np.where(differ, -1, pa), np.where(pa >= 0, pa, pb))
            p[r][g, :, b] = np.where(clash, np.where(differ, -1, pb), s[r][g, :, b])
    return {"yp": p.reshape(N, 128, A).astype(np.float32)}

@@ -1,0 +1,658 @@
+from concourse.bass import DstId, RemoteDMATransfer
+from concourse.mybir import AluOpType, AxisListType, ActivationFunctionType
+
+OP = AluOpType
+AF = ActivationFunctionType
+NR, W = 8, 4096
+MAGIC = 25165824.0
+
+f32, b16, h16, i32, u16 = "float32", "bfloat16", "float16", "int32", "uint16"
+SCRATCH = {}
+for _d, _l in (
+        (b16, "TZ 32768 F 8192 F0 2064 X 4096 Z0 1024 Z1 1024 VF 2048 VA 2048 MX 2048 MN 2048 EREP 2048 SB 4096 Y 4096 RM 1024 R255 1024 "
+              "BOB 128 IB 128 IBN 128 WD 144 MK 64 PC1 64 PC2 256 W1L 1024 W2L 1024 C2 128 E20 64 E21 64 E1 128 CLE 128"),
+        (h16, "TPH 256 PERM 512 NMO 256 NM 256 NMT 256 SW 272 HWO 4 HWN 64 BOH 128 BOK 128 IH 128 WS 144 RCA 1024 RCB 1024 RC 1024 CB 1024 "
+              "A16 128 CW 128 KX 1024 HGD 128 HTS 128 KBX 128"),
+        (i32, "TPI 128 SDI 128 HWI 3 THI 1 IP 16 IC 256 IC15 256 ICG 128 C48 64 L0T 128 S2 128 UI 16 UA 16 PP 8 VI 16 HI 128 HM 256 KI 16 "
+              "KFI 64 S1 128 NP1 128 NP2 128 KBI 8"),
+        (u16, "EL 64 REP 8 REP4 4 LL 256 LE 128 LH 256 LP 16 LN 8 LF 8 LPI 8"),
+        (f32, "COL 32 DL 128 RU 128 RB 64 CWT 128 C128 128 CT 8 CTT 8 CBC 8 SG 128 NMX 8 W1F 8 W2F 8 KCF 8 THK 8 KC 1024 SDV 128 S0M 128 "
+              "US 256 KK 128 HC 272 KS 256 CS 128 E2M 128 HIM 128 SUM 128 NFT 8 KB 8 KRS 128 KRP 128 PR 1024 YO 128")):
+    _l = _l.split()
+    for _i in range(0, len(_l), 2):
+        SCRATCH[_l[_i]] = ("sbuf", [128, int(_l[_i + 1])], _d)
+BANKS = ("BK0", "BK1", "PK0", "PK1", "HS", "KA", "VP0", "VP1")
+for _n in BANKS:
+    SCRATCH[_n] = ("psum", [128, 512], f32)
+SEMAPHORES = ["v", "s", "t", "gp", "nm", "hn", "ft", "fs", "ls", "hz0", "hz1"] + ["d%d" % i for i in range(20)] + \
+    ["ta%d" % q for q in range(NR)] + ["tb%d" % q for q in range(NR)]
+
+
+def mask_of(engs):
+    return sum(1 << e for e in engs)
+
+
+def places(T, topo):
+    chips, relay, used = [], {}, []
+    for r, c in enumerate(T.cores):
+        if not chips or topo.chip(T.cores[chips[-1][0]]) != topo.chip(c):
+            chips.append([])
+        chips[-1].append(r)
+        relay[r] = [x for x in topo.cores_of(c) if x not in T.cores and x not in used and topo.die(x) != topo.die(c)
+                    and all(topo.may_write(x, d) for d in T.cores)][0]
+        used.append(relay[r])
+    return chips, relay
+
+
+def rank_program(g, core, T, topo):
+    chips, relay = places(T, topo)
+    ncl = len(chips)
+    ls = [0]
+
+    def targets(r):
+        n = [i for i in range(ncl) if r in chips[i]][0]
+        return [T.cores[chips[(n - 1 - d) % ncl][-1]] for d in range(ncl - 1)]
+
+    def send(dst, lo, hi, sem, engs):
+        rid, pid = topo.addr(dst)[:2]
+        g.remote_dma(T.TZ[:, lo:hi], T.TZ[:, lo:hi], T.sem[sem], T.sem.ls, pid, rid, mask_of(engs))
+        ls[0] += len(engs)
+
+    rank = T.rank_of(core)
+    H2, Q4 = W // 2, W // 4
+    if rank is None:
+        for r in range(NR):
+            if relay[r] == core:
+                for n, d in enumerate(targets(r)):
+                    for i in range(2):
+                        if n == 0:
+                            g.wait_ge(T.sem["hz%d" % i], 8)
+                        o = r * W + H2 + i * Q4
+                        send(d, o, o + Q4, "tb%d" % r, topo.engines(core, d)[:8])
+                g.wait_ge(T.sem.ls, ls[0])
+        return
+
+    Q = {"v": g.vector, "s": g.scalar, "t": g.tensor, "g": g, "y": g.sync}
+    SEM = {"v": "v", "s": "s", "t": "t", "g": "gp"}
+    cnt = {e: 0 for e in SEM}
+    clk = {e: {} for e in Q}
+    hist, lastw, readers, ndma = {}, {}, {}, [0]
+
+    def wait(e, need):
+        for s, n in sorted(need.items()):
+            if clk[e].get(s, 0) < n:
+                Q[e].wait_ge(T.sem[s], n)
+                for s2, n2 in hist.get((s, n), {}).items():
+                    clk[e][s2] = max(clk[e].get(s2, 0), n2)
+                clk[e][s] = max(clk[e].get(s, 0), n)
+
+    def deps(e, R, Wt):
+        toks = [k for tg in R for k in lastw.get(tg, ())]
+        toks += [k for tg in R if tg in BANKS for k in readers.get(tg, {}).items() if k[0] != SEM.get(e)]
+        toks += [k for tg in Wt for k in lastw.get(tg, ()) if not (e == "t" and k[0] == "t")]
+        toks += [k for tg in Wt for k in readers.get(tg, {}).items() if k[0] != SEM.get(e)]
+        need = {}
+        for s, n in toks:
+            need[s] = max(need.get(s, 0), n)
+        return need
+
+    def done(tok, R, Wt):
+        for tg in R:
+            readers.setdefault(tg, {})[tok[0]] = tok[1]
+        for tg in Wt:
+            lastw[tg] = [tok]
+            readers[tg] = {}
+
+    def op(e, fn, R, Wt):
+        wait(e, deps(e, R, Wt))
+        ins = fn()
+        for i in (ins if isinstance(ins, list) else [ins]):
+            i.then_inc(T.sem[SEM[e]], 1)
+            cnt[e] += 1
+            hist[(SEM[e], cnt[e])] = dict(clk[e])
+        done((SEM[e], cnt[e]), R, Wt)
+
+    def dma(e, out, in_, R, Wt):
+        wait(e, deps(e, R, Wt))
+        s = "d%d" % ndma[0]
+        ndma[0] += 1
+        Q[e].dma_start(out, in_).then_inc(T.sem[s], 16)
+        hist[(s, 16)] = dict(clk[e])
+        done((s, 16), R, Wt)
+
+    V, S, PE = g.vector, g.scalar, g.tensor
+    mm = PE.matmul
+
+    def ts(out, a, s1, o1, R, Wt, s2=None, o2=None):
+        if o2 is None:
+            op("v", lambda: V.tensor_scalar(out, a, s1, None, o1), R, Wt)
+        else:
+            op("v", lambda: V.tensor_scalar(out, a, s1, s2, o1, o2), R, Wt)
+
+    def tt(out, a, b, o, R, Wt):
+        op("v", lambda: V.tensor_tensor(out, a, b, o), R, Wt)
+
+    def cp(out, a, R, Wt):
+        op("v", lambda: V.tensor_copy(out, a), R, Wt)
+
+    def fill(ap, x, Wt):
+        op("v", lambda: V.memset(ap, x), [], Wt)
+
+    def scan(out, d0, d1, o0, o1, R, Wt):
+        op("v", lambda: V.tensor_tensor_scan(out, d0, d1, 0.0, o0, o1), R, Wt)
+
+    def act(out, a, R, Wt, func=AF.Copy, bias=0.0, scale=1.0):
+        op("s", lambda: S.activation(out, a, func, bias=bias, scale=scale), R, Wt)
+
+    z0 = rank * W
+    dma("y", T.TPI[:], T.tp[:], [], ["TPI"])
+    dma("s", T.SDI[:], T.sd[:], [], ["SDI"])
+    dma("y", T.HWI[:], T.hw[:], [], ["HWI"])
+    dma("s", T.THI[:], T.th[:], [], ["THI"])
+    dma("y", T.TZ[:, z0:z0 + H2], T.tz[:, 0:H2], [], ["TZa%d" % rank])
+    dma("s", T.TZ[:, z0 + H2:z0 + W], T.tz[:, H2:W], [], ["TZb%d" % rank])
+    op("g", lambda: g.iota(T.IP[:, 0:1], [[0, 1]], 0, 1), [], ["IP"])
+    op("g", lambda: g.iota(T.IC[:], [[1, 256]], 0, 0), [], ["IC"])
+
+    C = {}
+    ip = {"P": T.IP[:, 0:1]}
+
+    def icol(name, *a):
+        n = len(ip)
+        ip[name] = T.IP[:, n:n + 1]
+        ts(ip[name], ip["P"], a[0], a[1], ["IP"], ["i" + name], *a[2:])
+
+    def col(name, src, s1, o1, s2=None, o2=None, R=()):
+        i = len(C)
+        C[name] = T.COL[:, i:i + 1]
+        ts(C[name], src, s1, o1, ["IP"] + ["i" + x for x in ip] + list(R), ["c" + name], s2, o2)
+
+    AND, SHR = OP.bitwise_and, OP.arith_shift_right
+    icol("K", 15, AND)
+    icol("Q", 14, AND)
+    icol("S", 1, AND)
+    icol("G", 4, SHR)
+    icol("B3", 3, SHR, 1, AND)
+    icol("B4", 4, SHR, 1, AND)
+    icol("B5", 5, SHR)
+    icol("L", 7, AND)
+    col("S8", ip["S"], 8.0, OP.mult)
+    col("G8", ip["G"], 1.0, OP.mult)
+    col("PM0", ip["Q"], 16.0, OP.mult, C["S8"], OP.add, ["cS8"])
+    col("PM", C["PM0"], C["G8"], OP.add, None, None, ["cPM0", "cG8"])
+    col("P", ip["P"], 1.0, OP.mult)
+    ts(T.PERM[:, 0:256], T.IC[:], C["PM"], OP.is_equal, ["IC", "cPM"], ["PERM0"])
+    ts(T.PERM[:, 256:512], T.IC[:], -16.0, OP.add, ["IC", "cPM"], ["PERM1"], C["PM"], OP.is_equal)
+    ts(T.IH[:], T.IC[:, 0:128], C["P"], OP.is_equal, ["IC", "cP"], ["IH"])
+    ts(T.TPH[:, 0:128], T.TPI[:], -2047.0, OP.add, ["TPI"], ["TPH0"])
+    ts(T.TPH[:, 128:256], T.SDI[:], -2047.0, OP.add, ["SDI"], ["TPH1"])
+
+    def turn():
+        mm(T.HS[:, 0:256], T.TPH[:, 0:128], T.PERM[:, 0:256], True, False)
+        return mm(T.HS[:, 0:256], T.TPH[:, 128:256], T.PERM[:, 256:512], False, True)
+    op("t", turn, ["TPH0", "TPH1", "PERM0", "PERM1"], ["HS"])
+    cp(T.HWO[:, 0:3], T.HWI[:], ["HWI"], ["HWO0"])
+    ts(T.HWO[:, 3:4], T.THI[:], -2048.0, OP.add, ["THI"], ["HWO1"])
+    cp(T.NMO[:], T.HS[:, 0:256], ["HS"], ["NMO"])
+    cp(T.NM[:, rank * 32:rank * 32 + 32], T.NMO[:, rank * 32:rank * 32 + 32], ["NMO"], ["NMo"])
+    cp(T.HWN[:, rank * 8:rank * 8 + 4], T.HWO[:], ["HWO0", "HWO1"], ["HWo"])
+
+    mine = [c for c in chips if rank in c][0]
+    far = [r for r in range(NR) if r not in mine]
+    near = [r for r in mine if r != rank][0]
+    others = far + [near]
+    last = rank == mine[-1]
+    fe = topo.engines(core, T.cores[far[0]])
+    ne = [e for e in topo.engines(core, T.cores[near]) if e not in fe]
+    slots = fe[:6] + [fe[6]] if last else fe[4:] + fe[4:6] + [ne[0]]
+
+    def did(r):
+        a = topo.addr(T.cores[r])
+        return DstId(rid=a[0], pnc=a[1])
+
+    def spread(src, dst, sem, engs):
+        todo = [(r, e) for r, e in zip(others, engs)]
+        while todo:
+            tr, seen, rest = [], [], []
+            for r, e in todo:
+                if e in seen:
+                    rest.append((r, e))
+                else:
+                    seen.append(e)
+                    tr.append(RemoteDMATransfer(dst_ids=[did(r)], dma_engine_mask=1 << e, remote_sem=T.sem[sem], srcs=[src(r)], dsts=[dst]))
+            g.remote_dma_fused(tr, local_sem=T.sem.ls)
+            ls[0] += len(tr)
+            todo = rest
+
+    wait("g", deps("g", ["NMO"], []))
+    spread(lambda r: T.NMO[:, r * 32:r * 32 + 32], T.NM[:, rank * 32:rank * 32 + 32], "nm", fe)
+    wait("g", deps("g", ["HWO0", "HWO1"], []))
+    g.remote_dma_fused([RemoteDMATransfer(dst_ids=[did(r) for r in others], dma_engine_mask=1 << fe[7], remote_sem=T.sem.hn, srcs=[T.HWO[:]],
+                                          dsts=[T.HWN[:, rank * 8:rank * 8 + 4] for _ in others])], local_sem=T.sem.ls)
+    ls[0] += 1
+    lastw["NM"], lastw["HWN"] = [("nm", 7)], [("hn", 7)]
+
+    def direct(d, engs):
+        wait("g", deps("g", ["TZa%d" % rank], []))
+        for i in range(8 // len(engs)):
+            n = H2 * len(engs) // 8
+            send(d, z0 + i * n, z0 + i * n + n, "ta%d" % rank, engs)
+
+    def to_relay():
+        wait("g", deps("g", ["TZb%d" % rank], []))
+        for i in range(2):
+            send(relay[rank], z0 + H2 + i * Q4, z0 + H2 + (i + 1) * Q4, "hz%d" % i, ne[:8])
+
+    def hand_on(q):
+        for h, x in enumerate("ab"):
+            wait("g", deps("g", ["TZ%s%d" % (x, q)], []))
+            send(T.cores[near], q * W + h * H2, q * W + (h + 1) * H2, "t%s%d" % (x, q), ne)
+
+    if last:
+        hand_on(rank)
+    else:
+        direct(targets(rank)[0], fe[:4])
+        to_relay()
+    ntb = {q: 16 if last and q in far else 8 for q in range(NR)}
+    for q in range(NR):
+        if q != rank:
+            lastw["TZa%d" % q] = [("ta%d" % q, 8)]
+            lastw["TZb%d" % q] = [("tb%d" % q, ntb[q])]
+
+    col("K", ip["K"], 1.0, OP.mult)
+    col("PG", ip["G"], 16.0, OP.mult)
+    col("PGF", C["PG"], 15.0, OP.add, None, None, ["cPG"])
+    col("QB", ip["Q"], 512.0, OP.mult)
+    col("S128", ip["S"], 128.0, OP.mult)
+    col("E0", ip["K"], 0.0, OP.is_equal)
+    col("E1", ip["K"], 1.0, OP.is_equal, 2048.0, OP.mult)
+    col("J128", ip["K"], 128.0, OP.mult)
+    col("B3", ip["B3"], 8.0, OP.add)
+    col("R2", ip["B5"], 2.0, OP.mult, C["B3"], OP.add, ["cB3"])
+    col("SW", ip["L"], 16.0, OP.mult, C["R2"], OP.add, ["cR2"])
+    col("T1", ip["B4"], 1.0, OP.mult)
+    col("T0", ip["B4"], 0.0, OP.is_equal)
+    ic = T.IC[:, 0:128]
+    for ty in range(2):
+        ts(T.SW[:, ty * 136:ty * 136 + 136], T.IC[:, 0:136], C["SW"], OP.is_equal, ["IC", "cSW", "cT%d" % ty], ["SW%d" % ty], C["T%d" % ty], OP.mult)
+    fill(T.F0[:, 2048:2064], -256.0, ["F0e"])
+    ts(T.L0T[:], ic, C["J128"], OP.add, ["IC", "cJ128"], ["L0T"])
+    pr = [T.PR[:, i * 128:i * 128 + 128] for i in range(8)]
+    ts(pr[0], T.TPI[:], 0.0, OP.is_lt, ["TPI"], ["pr0"], 2048.0, OP.mult)
+    tt(pr[1], T.L0T[:], pr[0], OP.max, ["L0T", "pr0"], ["pr1"])
+    cp(T.LE[:], pr[1], ["pr1"], ["LE"])
+    for b, (x, y) in enumerate(((0.0, 1.0), (255.0, 0.0))):
+        rm = (T.RM, T.R255)[b]
+        fill(rm[:], y, ["RM%d" % b])
+        fill(rm[:, 0::16], x, ["RM%d" % b])
+    fill(T.RU[:], 0.0, ["RU"])
+    fill(T.RU[:, 0::16], -1e9, ["RU"])
+    fill(T.RB[:], 0.0, ["RB"])
+    fill(T.RB[:, 0::16], 1e9, ["RB"])
+    op("t", lambda: [mm(T.HS[:, b * 128:b * 128 + 128], T.NM[:, b * 128:b * 128 + 128], T.IH[:], True, True) for b in range(2)],
+       ["NM", "NMo", "IH"], ["HS"])
+    cp(T.NMT[:], T.HS[:, 0:256], ["HS"], ["NMT"])
+
+    def back():
+        out = []
+        for ty in range(2):
+            o = T.KA[:, ty * 128:ty * 128 + 128]
+            mm(o, T.SW[:, ty * 136 + 8:ty * 136 + 136], T.NMT[:, 0:128], True, False)
+            out.append(mm(o, T.SW[:, ty * 136:ty * 136 + 128], T.NMT[:, 128:256], False, True))
+        return out
+    op("t", back, ["SW0", "SW1", "NMT"], ["KA"])
+    ts(T.LL[:], T.KA[:, 0:256], 2047.0, OP.add, ["KA"], ["LL"], 0.0, OP.max)
+    tzo = ["TZa%d" % rank, "TZb%d" % rank]
+
+    def feats(ty):
+        y0 = ty * 2048
+        win = T.TZ[:, z0:z0 + W]
+        act(T.Y[:, y0:y0 + 1024], win.indirect(T.LL[:, ty * 128:ty * 128 + 64]), tzo + ["LL"], ["Ya%d" % ty])
+        cp(T.Y[:, y0 + 1024:y0 + 2048], win.indirect(T.LL[:, ty * 128 + 64:ty * 128 + 128]), tzo + ["LL"], ["Yb%d" % ty])
+        for r in others + [rank]:
+            for s in range(2):
+                src = T.Y[:, y0 + 2 * r + s:y0 + 2048:16]
+                o = r * 512 + ty * 256 + s * 128
+                out, tag = T.SB[:, o:o + 128], "SB%d_%d_%d" % (r, ty, s)
+                if r == rank and ty == 0:
+                    out, tag = T.F0[:, rank * 256 + s * 128:rank * 256 + s * 128 + 128], "F0o%d" % s
+                elif r == rank:
+                    o = rank * 1024 + 256 + s * 128
+                    out, tag = T.F[:, o:o + 128], "Fso%d" % s
+                (cp if s == 0 else act)(out, src, ["Ya%d" % ty, "Yb%d" % ty], [tag])
+        wait("g", deps("g", ["SB%d_%d_%d" % (r, ty, s) for r in others for s in range(2)], []))
+        d = T.F0[:, rank * 256:rank * 256 + 256] if ty == 0 else T.F[:, rank * 1024 + 256:rank * 1024 + 512]
+        spread(lambda r: T.SB[:, r * 512 + ty * 256:r * 512 + ty * 256 + 256], d, "fs" if ty else "ft", slots)
+        lastw["Fsr" if ty else "F0r"] = [("fs" if ty else "ft", 7)]
+
+    feats(0)
+    feats(1)
+    f0 = ["F0r", "F0o0", "F0o1", "F0e"]
+    if last:
+        direct(targets(rank)[0], fe)
+        to_relay()
+    for d in targets(rank)[1:]:
+        direct(d, fe)
+    if not last:
+        hand_on(rank)
+    else:
+        n = [i for i in range(ncl) if rank in chips[i]][0]
+        for d in range(1, ncl):
+            for q in chips[(n + d) % ncl]:
+                hand_on(q)
+
+    ts(T.IC15[:], T.IC[:], 15, AND, ["IC"], ["IC15"])
+    ts(T.ICG[:], ic, 112, AND, ["IC"], ["ICG"])
+    ts(T.C48[:], T.IC[:, 0:64], 48, AND, ["IC"], ["C48"])
+    ts(T.EL[:], T.C48[:], C["K"], OP.add, ["C48", "cK"], ["EL"])
+    ts(T.MK[:], T.IC15[:, 0:64], C["K"], OP.not_equal, ["IC15", "cK"], ["MK"], -4194304.0, OP.mult)
+    ts(T.IB[:], ic, C["P"], OP.is_equal, ["IC", "cP"], ["IB"])
+    ts(T.IBN[:], ic, C["P"], OP.is_equal, ["IC", "cP"], ["IBN"], -1.0, OP.mult)
+    ts(T.DL[:], T.IC15[:, 0:128], C["K"], OP.is_equal, ["IC15", "cK"], ["DL"])
+    ts(T.BOB[:], T.ICG[:], C["PG"], OP.is_equal, ["ICG", "cPG"], ["BOB"])
+    ts(T.BOH[:], T.ICG[:], C["PG"], OP.is_equal, ["ICG", "cPG"], ["BOH"])
+    ts(T.BOK[:], T.ICG[:], C["PG"], OP.is_equal, ["ICG", "cPG"], ["BOK"], 1024.0, OP.mult)
+    cp(T.REP[:], T.IC[:, 0:8], ["IC"], ["REP"])
+    cp(T.REP4[:], T.IC[:, 4:8], ["IC"], ["REP4"])
+    ts(T.WD[:], T.IC[:, 0:144], C["PGF"], OP.is_equal, ["IC", "cPGF"], ["WD"], 4096.0, OP.mult)
+    ts(T.WS[:], T.IC[:, 0:144], C["PGF"], OP.is_equal, ["IC", "cPGF"], ["WS"], 1024.0, OP.mult)
+    ts(T.PC1[:], T.IC15[:, 0:64], 16.0, OP.mult, ["IC15", "cK"], ["PC1"], C["K"], OP.add)
+    for i in range(4):
+        ts(T.PC2[:, i * 64:i * 64 + 64], T.C48[:], 16.0, OP.mult, ["C48"], ["PC2%d" % i], 1024.0 * i, OP.add)
+    hwn = ["HWN", "HWo"]
+    for i, x in enumerate((T.W1F, T.W2F, T.KCF)):
+        cp(x[:], T.HWN[:, i::8], hwn, ["hw%d" % i])
+    ts(T.THK[:], T.HWN[:, 3::8], 2048.0, OP.add, hwn, ["THK"], 4096.0, OP.mult)
+    for t in range(NR):
+        q = (rank + 1 + t) % NR
+        o = slice(q * 128, q * 128 + 128)
+        ts(T.W1L[:, o], T.BOB[:], T.W1F[:, q:q + 1], OP.mult, ["BOB", "hw0"], ["W1L%d" % q], 0.5, OP.mult)
+        ts(T.W2L[:, o], T.BOB[:], T.W2F[:, q:q + 1], OP.mult, ["BOB", "hw1"], ["W2L%d" % q], 0.5, OP.mult)
+        ts(T.KX[:, o], T.DL[:], T.KCF[:, q:q + 1], OP.mult, ["DL", "hw2"], ["KX%d" % q])
+    for b in range(2):
+        op("t", lambda: mm(T["PK%d" % b][:], T.BOH[:], T.KX[:, b * 512:b * 512 + 512], True, True),
+           ["BOH"] + ["KX%d" % q for q in range(NR)], ["PK%d" % b])
+        act(T.KC[:, b * 512:b * 512 + 512], T["PK%d" % b][:], ["PK%d" % b], ["KC%d" % b])
+    for q in range(NR):
+        fill(T.F[:, q * 1024 + 512:(q + 1) * 1024], -256.0, ["FW%d" % q])
+    for h in range(2):
+        fill(T.E1[:, h * 64 + 48:h * 64 + 64], 0.0, ["E1z"])
+    ts(T.CWT[:], ic, 512.0, OP.add, ["IC"], ["CWT"], 1.0 / 1024, OP.mult)
+    ts(T.CW[:], T.CWT[:], C["E0"], OP.mult, ["CWT", "cE0", "cE1"], ["CW"], C["E1"], OP.add)
+    ts(T.C128[:], ic, 128.0, OP.add, ["IC"], ["C128"])
+    ts(T.CTT[:], T.IC[:, 0:8], 16.0, OP.mult, ["IC", "cK"], ["CTT"], C["K"], OP.add)
+    ts(T.CT[:], T.CTT[:], 256.0, OP.add, ["CTT"], ["CT"], 1.0 / 256, OP.mult)
+    ts(T.SG[:], ic, C["S128"], OP.add, ["IC", "cS128"], ["SG"])
+    ts(T.NMX[:], T.IC[:, 0:8], 2.0, OP.mult, ["IC", "cK"], ["NMX"], C["K"], OP.not_equal)
+    fill(T.HC[:, 256:272], -2048.0, ["HCe"])
+    for src, add, out, tag in ((T.TPI, 0.0, T.S2, "S2"), (T.SDI, 256.0, T.SDV, "SDV")):
+        ts(pr[2], src[:], 1.0, OP.add, ["TPI", "SDI"], ["pr2"], 1024.0, OP.mult)
+        tt(pr[3], pr[2], T.SG[:], OP.add, ["pr2", "SG"], ["pr3"])
+        ts(out[:], pr[3], add, OP.add, ["pr3"], [tag], 767.0, OP.max)
+    cp(T.A16[:], ic, ["IC"], ["A16"])
+    ts(T.CBC[:], T.IC[:, 0:8], C["G8"], OP.is_equal, ["IC", "cG8"], ["CBC"], -1024.0, OP.mult)
+    for c in range(8):
+        o = slice(c * 128, c * 128 + 128)
+        ts(T.RCA[:, o], ic, T.CTT[:, c:c + 1], OP.is_ge, ["IC", "CTT"], ["RCA%d" % c], 128.0, OP.mult)
+        ts(T.RCB[:, o], ic, T.CTT[:, c:c + 1], OP.is_equal, ["IC", "CTT"], ["RCB%d" % c], 128.0, OP.mult)
+        ts(T.CB[:, o], T.A16[:], 0.0, OP.mult, ["A16", "CBC"], ["CB%d_%d" % (c // 4, c % 4)], T.CBC[:, c:c + 1], OP.add)
+
+    def r_mm(b):
+        pk = T["PK%d" % b]
+        mm(pk[:], T.IH[:], T.RCA[:, b * 512:b * 512 + 512], True, False)
+        for c in range(4):
+            mm(pk[:, c * 128:c * 128 + 128], T.IH[:], T.A16[:], False, False)
+        return mm(pk[:], T.IH[:], T.RCB[:, b * 512:b * 512 + 512], False, True)
+    for b in range(2):
+        op("t", lambda: r_mm(b), ["IH", "A16"] + ["RC%s%d" % (x, c) for x in "AB" for c in range(8)], ["PK%d" % b])
+        cp(T.RC[:, b * 512:b * 512 + 512], T["PK%d" % b][:], ["PK%d" % b], ["RC%d" % b])
+    for q in range(NR):
+        dma("y", T.F[:, q * 1024:q * 1024 + 256], T.F0[:, q * 256:q * 256 + 256], f0, ["Ft%d" % q])
+    fall = ["Ft%d" % q for q in range(NR)] + ["FW%d" % q for q in range(NR)] + ["Fsr", "Fso0", "Fso1"]
+
+    def run(*gens):
+        gens = list(gens)
+        while gens:
+            for x in list(gens):
+                try:
+                    next(x)
+                except StopIteration:
+                    gens.remove(x)
+
+    bk = [T.BK0, T.BK1]
+
+    def u_mm(q, h, src, tag):
+        o = slice(q * 128, q * 128 + 128)
+
+        def f():
+            out = []
+            for u, wl in enumerate((T.W1L, T.W2L)):
+                mm(bk[h][:, u * 64:u * 64 + 64], T.IB[:], T.MK[:], True, False)
+                out.append(mm(bk[h][:, u * 64:u * 64 + 64], wl[:, o], src, False, True))
+            return out
+        op("t", f, ["IB", "MK", "W1L%d" % q, "W2L%d" % q, tag], ["BK%d" % h])
+
+    def e_load(win, R):
+        act(T.VF[:, 0:1024], win.indirect(T.LE[:, 0:64]), R + ["LE"], ["VF0"])
+        cp(T.VF[:, 1024:2048], win.indirect(T.LE[:, 64:128]), R + ["LE"], ["VF1"])
+        for h in range(2):
+            o = slice(h * 1024, h * 1024 + 1024)
+            scan(T.MX[:, o], T.RM[:], T.VF[:, o], OP.mult, OP.max, ["RM0", "VF%d" % h], ["MX%d" % h])
+            act(T.VA[:, o], T.VF[:, o], ["VF%d" % h], ["VA%d" % h], AF.Abs)
+            act(T.HIM[:, h * 64:h * 64 + 64], T.MX[:, h * 1024 + 15:h * 1024 + 1024:16], ["MX%d" % h], ["HIM%d" % h], AF.Identity, bias=-0.5)
+
+    def e_gen(h, q):
+        o = slice(h * 1024, h * 1024 + 1024)
+        hh = slice(h * 64, h * 64 + 64)
+        scan(T.MN[:, o], T.R255[:], T.VA[:, o], OP.max, OP.min, ["RM1", "VA%d" % h], ["MN%d" % h])
+        yield
+        tt(T.SUM[:, hh], T.HIM[:, hh], T.MN[:, h * 1024 + 15:h * 1024 + 1024:16], OP.add, ["HIM%d" % h, "MN%d" % h], ["SUM%d" % h])
+        yield
+        e2 = T["E2%d" % h]
+        tg = "E2%d" % h
+        ts(e2[:], T.SUM[:, hh], MAGIC, OP.add, ["SUM%d" % h], [tg], MAGIC, OP.subtract)
+        u_mm(q, h, e2[:], tg)
+        act(T.EREP[:, o], e2[:].indirect(T.EL[:]), [tg, "EL"], ["EREP%d" % h], scale=0.5)
+        b = h * 64
+        act(T.E2M[:, b:b + 48], e2[:, 0:48], [tg], ["E2Ma%d" % h], AF.Identity, bias=-0.5)
+        act(T.E2M[:, b + 48:b + 64], e2[:, 48:64], [tg], ["E2Mb%d" % h], AF.Identity, bias=-0.5, scale=0.5)
+        act(T.E1[:, b:b + 48], e2[:, 0:48], [tg, "E1z"], ["E1%d" % h], scale=0.5)
+        yield
+
+    def hash_gen(p, h, q):
+        x = "%d" % h
+        i = p * 2 + h
+        us, kk, hi = T.US[:, h * 128:h * 128 + 128], T.KK[:, h * 64:h * 64 + 64], T.HI[:, h * 64:h * 64 + 64]
+        ui, ua, pp, vi = T.UI[:, h * 8:h * 8 + 8], T.UA[:, h * 8:h * 8 + 8], T.PP[:, h * 4:h * 4 + 4], T.VI[:, h * 8:h * 8 + 4]
+        scan(us, T.RU[:], bk[h][:, 0:128], OP.add, OP.max, ["RU", "BK" + x], ["US" + x])
+        yield
+        cp(ui, T.US[:, h * 128 + 15:h * 128 + 128:16], ["US" + x], ["UI" + x])
+        yield
+        ts(ua, ui, 4095, AND, ["UI" + x], ["UA" + x])
+        yield
+        tt(pp, T.UA[:, h * 8:h * 8 + 4], T.UA[:, h * 8 + 4:h * 8 + 8], OP.mult, ["UA" + x], ["PP" + x])
+        tt(kk, ua.indirect(T.REP4[:]), T.KC[:, q * 128:q * 128 + 64], OP.mult, ["UA" + x, "REP4", "KC%d" % (q // 4)], ["KK" + x])
+        yield
+        ts(vi, pp, 5, SHR, ["PP" + x], ["VI" + x])
+        yield
+        tt(hi, vi.indirect(T.REP[:, 0:4]), kk, OP.add, ["VI" + x, "KK" + x, "REP"], ["HI" + x])
+        yield
+        hm = T.HM[:, i * 64:i * 64 + 64]
+        ts(hm, hi, 4095, AND, ["HI" + x], ["HM%d" % i])
+        yield
+        cp(T.LH[:, i * 64:i * 64 + 64], hm, ["HM%d" % i], ["LH%d" % i])
+        yield
+
+    def cand(p, h, q, n=1):
+        i = p * 2 + h
+        x0, l0, e0 = i * 1024, i * 64, h * 1024
+        tz = T.TZ[:, q * W:q * W + W]
+        R = ["TZa%d" % q, "TZb%d" % q, "LH%d" % i]
+        zb, xp = T["Z%d" % h], T["VP%d" % h][:, 0:256]
+        act(T.X[:, x0 + 768:x0 + 1024], tz.indirect(T.LH[:, l0 + 48:l0 + 64]), R, ["X%d_r" % i])
+
+        def f():
+            mm(xp, T.IB[:], T.X[:, x0 + 768:x0 + 1024], True, False)
+            return mm(xp, T.IBN[:], T.EREP[:, e0 + 768:e0 + 1024], False, True)
+        op("t", f, ["IB", "IBN", "X%d_r" % i, "EREP%d" % h], ["VP%d" % h])
+        w = 768 // n
+        for j in range(n):
+            o = j * w
+            tt(T.X[:, x0 + o:x0 + o + w], tz.indirect(T.LH[:, l0 + o // 16:l0 + (o + w) // 16]), T.EREP[:, e0 + o:e0 + o + w],
+               OP.subtract, R + ["EREP%d" % h], ["X%d_%d" % (i, j)])
+            act(zb[:, o:o + w], T.X[:, x0 + o:x0 + o + w], ["X%d_%d" % (i, j)], ["Z%d_%d" % (h, j)], AF.Abs)
+            if j == 0:
+                act(zb[:, 768:1024], xp, ["VP%d" % h], ["Z%d_r" % h], AF.Abs)
+
+    def dist(p, h):
+        i = p * 2 + h
+        zb = T["Z%d" % h]
+        key = bk[h][:, 128:192]
+
+        def f():
+            mm(key, T.IB[:], T.PC1[:], True, False)
+            r_ = mm(key, T.IB[:], T.PC2[:, i * 64:i * 64 + 64], False, False)
+            for k in range(16):
+                r_ = mm(key, T.WD[:, 15 - k:143 - k], zb[:, k::16], False, k == 15)
+            return r_
+        op("t", f, ["IB", "PC1", "PC2%d" % i, "WD", "Z%d_0" % h, "Z%d_1" % h, "Z%d_r" % h], ["BK%d" % h])
+
+    def names(p, h):
+        i = p * 2 + h
+        ts(T.HC[:, i * 64:i * 64 + 64], T.HM[:, i * 64:i * 64 + 64], -2047.0, OP.add, ["HM%d" % i], ["HC%d" % i])
+
+    def best(p, h):
+        i = p * 2 + h
+        scan(T.KS[:, i * 64:i * 64 + 64], T.RB[:], bk[h][:, 128:192], OP.max, OP.min, ["RB", "BK%d" % h], ["KS%d" % i])
+
+    def arg_gen(h, q):
+        x = "%d" % h
+        hh = slice(h * 64, h * 64 + 64)
+        best(0, h)
+        yield
+        ki = T.KI[:, h * 8:h * 8 + 4]
+        ka = T.KI[:, h * 8 + 4:h * 8 + 8]
+        cp(ki, T.KS[:, h * 64 + 15:h * 64 + 64:16], ["KS" + x], ["KI" + x])
+        yield
+        ts(ka, ki, 1023, AND, ["KI" + x], ["KA_" + x])
+        yield
+        lp = T.LP[:, h * 8:h * 8 + 4]
+        cp(lp, ka, ["KA_" + x], ["LP" + x])
+        yield
+        tt(T.CS[:, hh], T.X[:, h * 1024:h * 1024 + 1024].indirect(lp), T.E2M[:, hh], OP.add,
+           ["X%s_0" % x, "X%s_r" % x, "LP" + x, "E2Ma" + x, "E2Mb" + x], ["CS" + x])
+        yield
+        ts(T.C2[:, hh], T.CS[:, hh], MAGIC, OP.add, ["CS" + x], ["C2" + x], MAGIC, OP.subtract)
+        u_mm(q, h, T.C2[:, hh], "C2" + x)
+        yield
+
+    for t in range(NR):
+        q = (rank + 1 + t) % NR
+        if t == 0:
+            e_load(T.F0[:, 0:2064], f0)
+        else:
+            e_load(T.F[:], fall)
+        run(e_gen(0, q))
+        run(e_gen(1, q), hash_gen(0, 0, q))
+        cand(0, 0, q)
+        dist(0, 0)
+        run(hash_gen(0, 1, q))
+        cand(0, 1, q)
+        run(arg_gen(0, q))
+        for b in range(2):
+            op("t", lambda: mm(T["PK%d" % b][:], T.IH[:], T.RC[:, b * 512:b * 512 + 512], True, False), ["IH", "RC%d" % b], ["PK%d" % b])
+        dist(0, 1)
+        names(0, 0)
+        run(hash_gen(1, 0, q))
+        cand(1, 0, q)
+        run(arg_gen(1, q))
+        dist(1, 0)
+        names(0, 1)
+        run(hash_gen(1, 1, q))
+        cand(1, 1, q, 2)
+        dist(1, 1)
+        best(1, 0)
+        names(1, 0)
+        names(1, 1)
+        ts(T.S0M[:], T.S2[:], T.NMX[:, q:q + 1], OP.mult, ["S2", "NMX"], ["S0M"], 767.0, OP.max)
+        best(1, 1)
+        kf, nf, ps, pm, kl, pia = (T.KFI[:, i * 8:i * 8 + 8] for i in range(6))
+        tt(kf, T.KS[:, 15:128:16], T.KS[:, 143:256:16], OP.min, ["KS0", "KS1", "KS2", "KS3"], ["kf"])
+        ts(nf, kf, T.THK[:, q:q + 1], OP.is_ge, ["kf", "THK"], ["nf"], 256.0, OP.mult)
+        ts(ps, kf, 4095, AND, ["kf"], ["ps"], 4, SHR)
+        tt(pm, nf, ps, OP.max, ["nf", "ps"], ["pm"])
+        cp(T.LN[:], pm, ["pm"], ["LN"])
+        tt(T.HGD[:], T.HC[:].indirect(T.LN[:]), T.DL[:], OP.mult, ["HC0", "HC1", "HC2", "HC3", "HCe", "LN", "DL"], ["HGD"])
+        op("t", lambda: mm(T.HS[:, 0:128], T.HGD[:], T.IH[:], True, True), ["HGD", "IH"], ["HS"])
+
+        def sv():
+            wl = T.WS[:, 15 - 2 * q:143 - 2 * q]
+            mm(T.HS[:, 128:256], wl, T.CW[:], True, False)
+            return mm(T.HS[:, 128:256], wl, T.HGD[:], False, True)
+        op("t", sv, ["WS", "CW", "HGD"], ["HS"])
+        for b in range(2):
+            pk = T["PK%d" % b]
+            op("t", lambda: [mm(pk[:, c * 128:c * 128 + 128], T.BOK[:], T.HGD[:], False, False) for c in range(4)][-1],
+               ["BOK", "HGD"], ["PK%d" % b])
+            if b == 0:
+                cp(T.HTS[:], T.HS[:, 0:128], ["HS"], ["HTS"])
+            op("t", lambda: mm(pk[:], T.HTS[:], T.CB[:, b * 512:b * 512 + 512], False, True),
+               ["HTS"] + ["CB%d_%d" % (b, c) for c in range(4)], ["PK%d" % b])
+        tt(T.S1[:], T.HS[:, 128:256], T.S0M[:], OP.max, ["HS", "S0M"], ["S1"])
+        tt(T.NFT[:], nf, T.CT[:], OP.mult, ["nf", "CT"], ["NFT"])
+        ts(kl, kf, 4095, AND, ["kf"], ["kl"])
+        ts(T.NP1[:], T.S1[:], 10, SHR, ["S1"], ["NP1"])
+        cp(T.LF[:], kl, ["kl"], ["LF"])
+        ts(T.NP2[:], T.S1[:], 10, SHR, ["S1"], ["NP2"])
+        for c in range(8):
+            pk = T["PK%d" % (c // 4)]
+            op("v", lambda: V.tensor_reduce(T.KB[:, c:c + 1], pk[:, (c % 4) * 128:(c % 4) * 128 + 128], AxisListType.X, OP.min,
+                                            apply_absolute_value=True), ["PK%d" % (c // 4)], ["KB%d" % c])
+            if c == 3 and t < NR - 1:
+                tt(T.F[:, q * 1024 + 512:q * 1024 + 640], T.X[:].indirect(T.LF[:]), T.E1[:], OP.add,
+                   ["X%d_%s" % (i, j) for i in range(4) for j in "01r"] + ["LF", "E10", "E11", "E1z"], ["FW%d" % q])
+        tt(T.KBI[:], T.KB[:], T.NFT[:], OP.max, ["KB%d" % c for c in range(8)] + ["NFT"], ["KBI"])
+        tt(T.KBX[:], T.KBI[:].indirect(T.REP[:]), T.DL[:], OP.mult, ["KBI", "REP", "DL"], ["KBX"])
+        ts(pia, T.KBI[:], 127, AND, ["KBI"], ["pia"])
+        op("t", lambda: mm(T.KA[:, 0:128], T.BOH[:], T.KBX[:], True, True), ["BOH", "KBX"], ["KA"])
+        act(T.KRS[:], T.KA[:, 0:128], ["KA"], ["KRS"])
+        cp(T.LPI[:], pia, ["pia"], ["LPI"])
+        act(T.KRP[:], T.KRS[:].indirect(T.LPI[:]), ["KRS", "LPI"], ["KRP"])
+        sp, nq, mnn, cl, bm, dsb, alt, dd = pr
+        am, ef, sa, m_, ds, kep, k0, nan = (T["VP%d" % (i // 4)][:, (i % 4) * 128:(i % 4) * 128 + 128] for i in range(8))
+        tt(nq, T.NP1[:].indirect(T.LPI[:]), T.NP2[:], OP.not_equal, ["NP1", "NP2", "LPI"], ["nq"])
+        tt(mnn, T.NP1[:].indirect(T.LPI[:]), T.NP2[:], OP.min, ["NP1", "NP2", "LPI"], ["mnn"])
+        cp(sp, T.S1[:].indirect(T.LPI[:]), ["S1", "LPI"], ["sp"])
+        tt(cl, nq, mnn, OP.mult, ["nq", "mnn"], ["cl"])
+        ts(am, T.KRS[:], 128.0, OP.is_ge, ["KRS", "VP0"], ["am"])
+        tt(bm, T.KRP[:], T.C128[:], OP.is_equal, ["KRP", "C128"], ["bm"])
+        tt(ef, am, bm, OP.max, ["am", "bm"], ["ef"])
+        tt(T.CLE[:], cl, ef, OP.mult, ["cl", "ef"], ["CLE"])
+        op("t", lambda: mm(T.KA[:, 128:256], T.BOB[:], T.CLE[:], True, True), ["BOB", "CLE"], ["KA"])
+        tt(sa, sp, am, OP.mult, ["sp", "am"], ["sa"])
+        ts(kep, T.CLE[:], 0.0, OP.is_equal, ["CLE", "VP1"], ["kep"])
+        tt(m_, T.S1[:], sa, OP.max, ["S1", "sa"], ["m"])
+        tt(k0, T.S1[:], kep, OP.mult, ["S1", "kep"], ["k0"])
+        tt(ds, T.SDV[:], m_, OP.subtract, ["SDV", "m"], ["ds"])
+        ts(k0, k0, 767.0, OP.max, ["k0"], ["k0"])
+        tt(dsb, ds, bm, OP.mult, ["ds", "bm"], ["dsb"])
+        tt(alt, m_, dsb, OP.add, ["m", "dsb"], ["alt"])
+        tt(dd, alt, k0, OP.subtract, ["alt", "k0"], ["dd"])
+        ts(nan, T.KA[:, 128:256], 0.0, OP.is_equal, ["KA"], ["nan"])
+        tt(dsb, dd, nan, OP.mult, ["dd", "nan"], ["dsb"])
+        tt(T.S2[:], k0, dsb, OP.add, ["k0", "dsb", "VP0", "VP1"], ["S2"])
+        if t < NR - 1:
+            ts(T.L0T[:], T.S2[:], 1023, AND, ["S2"], ["L0T"])
+            ts(T.LE[:], T.L0T[:], C["QB"], OP.add, ["L0T", "cQB"], ["LE"])
+    ts(T.L0T[:], T.S2[:], 10, SHR, ["S2"], ["L0T"])
+    ts(T.YO[:], T.L0T[:], -1.0, OP.add, ["L0T"], ["YO"])
+    dma("y", T.yp[:], T.YO[:], ["YO"], ["yp"])
+
+    need = {"v": cnt["v"], "s": cnt["s"], "t": cnt["t"], "gp": cnt["g"], "ls": ls[0], "nm": 7, "hn": 7, "ft": 7, "fs": 7}
+    for i in range(ndma[0]):
+        need["d%d" % i] = 16
+    for q in range(NR):
+        if q != rank:
+            need["ta%d" % q] = 8
+            need["tb%d" % q] = ntb[q]
+    wait("y", need)

@@ -11,7 +11,7 @@ SCRATCH = {}
 for _d, _l in (
         (b16, "TZ 32768 F 8192 F0 2064 X 4096 Z0 1024 Z1 1024 VF 2048 VA 2048 MX 2048 MN 2048 EREP 2048 SB 4096 Y 4096 RM 1024 R255 1024 "
               "BOB 128 IB 128 IBN 128 WD 144 MK 64 PC1 64 PC2 256 W1L 1024 W2L 1024 C2 128 E20 64 E21 64 E1 128 CLE 128"),
-        (h16, "TPH 256 PERM 512 NMO 256 NM 256 NMT 256 SW 272 HWO 4 HWN 64 BOH 128 BOK 128 IH 128 WS 144 RCA 1024 RCB 1024 RC 1024 CB 1024 "
+        (h16, "TPH 256 PERM 512 NMO 256 NM 256 NMT 256 SW 272 HWO 4 HWN 64 BOH 128 BOK 128 IH 128 WS 144 RCA 1024 RCB 1024 CB 1024 "
               "A16 128 CW 128 KX 1024 HGD 128 HTS 128 KBX 128"),
         (i32, "TPI 128 SDI 128 HWI 3 THI 1 IP 16 IC 256 IC15 256 ICG 128 C48 64 L0T 128 S2 128 UI 16 UA 16 PP 8 VI 16 HI 128 HM 256 KI 16 "
               "KFI 64 S1 128 NP1 128 NP2 128 KBI 8"),
@@ -363,16 +363,17 @@ def rank_program(g, core, T, topo):
     for i, x in enumerate((T.W1F, T.W2F, T.KCF)):
         cp(x[:], T.HWN[:, i::8], hwn, ["hw%d" % i])
     ts(T.THK[:], T.HWN[:, 3::8], 2048.0, OP.add, hwn, ["THK"], 4096.0, OP.mult)
-    for t in range(NR):
-        q = (rank + 1 + t) % NR
+
+    def hash_consts(q):
         o = slice(q * 128, q * 128 + 128)
         ts(T.W1L[:, o], T.BOB[:], T.W1F[:, q:q + 1], OP.mult, ["BOB", "hw0"], ["W1L%d" % q], 0.5, OP.mult)
         ts(T.W2L[:, o], T.BOB[:], T.W2F[:, q:q + 1], OP.mult, ["BOB", "hw1"], ["W2L%d" % q], 0.5, OP.mult)
         ts(T.KX[:, o], T.DL[:], T.KCF[:, q:q + 1], OP.mult, ["DL", "hw2"], ["KX%d" % q])
-    for b in range(2):
-        op("t", lambda: mm(T["PK%d" % b][:], T.BOH[:], T.KX[:, b * 512:b * 512 + 512], True, True),
-           ["BOH"] + ["KX%d" % q for q in range(NR)], ["PK%d" % b])
-        act(T.KC[:, b * 512:b * 512 + 512], T["PK%d" % b][:], ["PK%d" % b], ["KC%d" % b])
+        op("t", lambda: mm(T.KA[:, 256:384], T.BOH[:], T.KX[:, o], True, True), ["BOH", "KX%d" % q], ["KA"])
+        act(T.KC[:, o], T.KA[:, 256:384], ["KA"], ["KC%d" % q])
+
+    for t in range(NR):
+        hash_consts((rank + 1 + t) % NR)
     for q in range(NR):
         fill(T.F[:, q * 1024 + 512:(q + 1) * 1024], -256.0, ["FW%d" % q])
     for h in range(2):
@@ -396,28 +397,22 @@ def rank_program(g, core, T, topo):
         ts(T.RCA[:, o], ic, T.CTT[:, c:c + 1], OP.is_ge, ["IC", "CTT"], ["RCA%d" % c], 128.0, OP.mult)
         ts(T.RCB[:, o], ic, T.CTT[:, c:c + 1], OP.is_equal, ["IC", "CTT"], ["RCB%d" % c], 128.0, OP.mult)
         ts(T.CB[:, o], T.A16[:], 0.0, OP.mult, ["A16", "CBC"], ["CB%d_%d" % (c // 4, c % 4)], T.CBC[:, c:c + 1], OP.add)
-
-    def r_mm(b):
-        pk = T["PK%d" % b]
-        mm(pk[:], T.IH[:], T.RCA[:, b * 512:b * 512 + 512], True, False)
-        for c in range(4):
-            mm(pk[:, c * 128:c * 128 + 128], T.IH[:], T.A16[:], False, False)
-        return mm(pk[:], T.IH[:], T.RCB[:, b * 512:b * 512 + 512], False, True)
-    for b in range(2):
-        op("t", lambda: r_mm(b), ["IH", "A16"] + ["RC%s%d" % (x, c) for x in "AB" for c in range(8)], ["PK%d" % b])
-        cp(T.RC[:, b * 512:b * 512 + 512], T["PK%d" % b][:], ["PK%d" % b], ["RC%d" % b])
     for q in range(NR):
         dma("y", T.F[:, q * 1024:q * 1024 + 256], T.F0[:, q * 256:q * 256 + 256], f0, ["Ft%d" % q])
     fall = ["Ft%d" % q for q in range(NR)] + ["FW%d" % q for q in range(NR)] + ["Fsr", "Fso0", "Fso1"]
 
     def run(*gens):
-        gens = list(gens)
-        while gens:
-            for x in list(gens):
-                try:
-                    next(x)
-                except StopIteration:
-                    gens.remove(x)
+        now, ready, rk = 0, [0] * len(gens), [0] * len(gens)
+        live = list(range(len(gens)))
+        while live:
+            i = min(live, key=lambda j: (max(ready[j], now), rk[j], j))
+            try:
+                cost, lat, rk[i] = next(gens[i])
+            except StopIteration:
+                live.remove(i)
+                continue
+            now = max(now, ready[i]) + cost
+            ready[i] = now + lat
 
     bk = [T.BK0, T.BK1]
 
@@ -433,21 +428,23 @@ def rank_program(g, core, T, topo):
         op("t", f, ["IB", "MK", "W1L%d" % q, "W2L%d" % q, tag], ["BK%d" % h])
 
     def e_load(win, R):
-        act(T.VF[:, 0:1024], win.indirect(T.LE[:, 0:64]), R + ["LE"], ["VF0"])
-        cp(T.VF[:, 1024:2048], win.indirect(T.LE[:, 64:128]), R + ["LE"], ["VF1"])
         for h in range(2):
-            o = slice(h * 1024, h * 1024 + 1024)
-            scan(T.MX[:, o], T.RM[:], T.VF[:, o], OP.mult, OP.max, ["RM0", "VF%d" % h], ["MX%d" % h])
-            act(T.VA[:, o], T.VF[:, o], ["VF%d" % h], ["VA%d" % h], AF.Abs)
-            act(T.HIM[:, h * 64:h * 64 + 64], T.MX[:, h * 1024 + 15:h * 1024 + 1024:16], ["MX%d" % h], ["HIM%d" % h], AF.Identity, bias=-0.5)
+            o, l = h * 1024, h * 64
+            act(T.VF[:, o:o + 512], win.indirect(T.LE[:, l:l + 32]), R + ["LE"], ["VFa%d" % h])
+            cp(T.VF[:, o + 512:o + 1024], win.indirect(T.LE[:, l + 32:l + 64]), R + ["LE"], ["VFb%d" % h])
+            act(T.VA[:, o:o + 1024], T.VF[:, o:o + 1024], ["VFa%d" % h, "VFb%d" % h], ["VA%d" % h], AF.Abs)
 
     def e_gen(h, q):
         o = slice(h * 1024, h * 1024 + 1024)
         hh = slice(h * 64, h * 64 + 64)
+        end = slice(h * 1024 + 15, h * 1024 + 1024, 16)
+        scan(T.MX[:, o], T.RM[:], T.VF[:, o], OP.mult, OP.max, ["RM0", "VFa%d" % h, "VFb%d" % h], ["MX%d" % h])
+        yield 500, 400, 0
+        ts(T.HIM[:, hh], T.MX[:, end], -0.5, OP.add, ["MX%d" % h], ["HIM%d" % h])
         scan(T.MN[:, o], T.R255[:], T.VA[:, o], OP.max, OP.min, ["RM1", "VA%d" % h], ["MN%d" % h])
-        yield
-        tt(T.SUM[:, hh], T.HIM[:, hh], T.MN[:, h * 1024 + 15:h * 1024 + 1024:16], OP.add, ["HIM%d" % h, "MN%d" % h], ["SUM%d" % h])
-        yield
+        yield 500, 180, 0
+        tt(T.SUM[:, hh], T.HIM[:, hh], T.MN[:, end], OP.add, ["HIM%d" % h, "MN%d" % h], ["SUM%d" % h])
+        yield 120, 180, 0
         e2 = T["E2%d" % h]
         tg = "E2%d" % h
         ts(e2[:], T.SUM[:, hh], MAGIC, OP.add, ["SUM%d" % h], [tg], MAGIC, OP.subtract)
@@ -457,7 +454,7 @@ def rank_program(g, core, T, topo):
         act(T.E2M[:, b:b + 48], e2[:, 0:48], [tg], ["E2Ma%d" % h], AF.Identity, bias=-0.5)
         act(T.E2M[:, b + 48:b + 64], e2[:, 48:64], [tg], ["E2Mb%d" % h], AF.Identity, bias=-0.5, scale=0.5)
         act(T.E1[:, b:b + 48], e2[:, 0:48], [tg, "E1z"], ["E1%d" % h], scale=0.5)
-        yield
+        yield 60, 700, 0
 
     def hash_gen(p, h, q):
         x = "%d" % h
@@ -465,25 +462,27 @@ def rank_program(g, core, T, topo):
         us, kk, hi = T.US[:, h * 128:h * 128 + 128], T.KK[:, h * 64:h * 64 + 64], T.HI[:, h * 64:h * 64 + 64]
         ui, ua, pp, vi = T.UI[:, h * 8:h * 8 + 8], T.UA[:, h * 8:h * 8 + 8], T.PP[:, h * 4:h * 4 + 4], T.VI[:, h * 8:h * 8 + 4]
         scan(us, T.RU[:], bk[h][:, 0:128], OP.add, OP.max, ["RU", "BK" + x], ["US" + x])
-        yield
+        yield 120, 180, 0
         cp(ui, T.US[:, h * 128 + 15:h * 128 + 128:16], ["US" + x], ["UI" + x])
-        yield
+        yield 60, 180, 0
         ts(ua, ui, 4095, AND, ["UI" + x], ["UA" + x])
-        yield
+        yield 60, 180, 0
         tt(pp, T.UA[:, h * 8:h * 8 + 4], T.UA[:, h * 8 + 4:h * 8 + 8], OP.mult, ["UA" + x], ["PP" + x])
-        tt(kk, ua.indirect(T.REP4[:]), T.KC[:, q * 128:q * 128 + 64], OP.mult, ["UA" + x, "REP4", "KC%d" % (q // 4)], ["KK" + x])
-        yield
+        tt(kk, ua.indirect(T.REP4[:]), T.KC[:, q * 128:q * 128 + 64], OP.mult, ["UA" + x, "REP4", "KC%d" % q], ["KK" + x])
+        yield 230, 120, 0
         ts(vi, pp, 5, SHR, ["PP" + x], ["VI" + x])
-        yield
+        yield 60, 180, 0
         tt(hi, vi.indirect(T.REP[:, 0:4]), kk, OP.add, ["VI" + x, "KK" + x, "REP"], ["HI" + x])
-        yield
+        yield 150, 180, 0
         hm = T.HM[:, i * 64:i * 64 + 64]
         ts(hm, hi, 4095, AND, ["HI" + x], ["HM%d" % i])
-        yield
+        yield 60, 180, 0
         cp(T.LH[:, i * 64:i * 64 + 64], hm, ["HM%d" % i], ["LH%d" % i])
-        yield
+        yield 60, 180, 1
 
-    def cand(p, h, q, n=1):
+    issued = []
+
+    def cand(p, h, q):
         i = p * 2 + h
         x0, l0, e0 = i * 1024, i * 64, h * 1024
         tz = T.TZ[:, q * W:q * W + W]
@@ -495,27 +494,34 @@ def rank_program(g, core, T, topo):
             mm(xp, T.IB[:], T.X[:, x0 + 768:x0 + 1024], True, False)
             return mm(xp, T.IBN[:], T.EREP[:, e0 + 768:e0 + 1024], False, True)
         op("t", f, ["IB", "IBN", "X%d_r" % i, "EREP%d" % h], ["VP%d" % h])
-        w = 768 // n
-        for j in range(n):
-            o = j * w
-            tt(T.X[:, x0 + o:x0 + o + w], tz.indirect(T.LH[:, l0 + o // 16:l0 + (o + w) // 16]), T.EREP[:, e0 + o:e0 + o + w],
-               OP.subtract, R + ["EREP%d" % h], ["X%d_%d" % (i, j)])
-            act(zb[:, o:o + w], T.X[:, x0 + o:x0 + o + w], ["X%d_%d" % (i, j)], ["Z%d_%d" % (h, j)], AF.Abs)
-            if j == 0:
-                act(zb[:, 768:1024], xp, ["VP%d" % h], ["Z%d_r" % h], AF.Abs)
-
-    def dist(p, h):
-        i = p * 2 + h
-        zb = T["Z%d" % h]
         key = bk[h][:, 128:192]
 
-        def f():
+        def keys():
             mm(key, T.IB[:], T.PC1[:], True, False)
-            r_ = mm(key, T.IB[:], T.PC2[:, i * 64:i * 64 + 64], False, False)
+            return mm(key, T.IB[:], T.PC2[:, i * 64:i * 64 + 64], False, False)
+        op("t", keys, ["IB", "PC1", "PC2%d" % i], ["BK%d" % h])
+        if h == 1:
+            first_dist(p)
+        tt(T.X[:, x0:x0 + 768], tz.indirect(T.LH[:, l0:l0 + 48]), T.EREP[:, e0:e0 + 768], OP.subtract, R + ["EREP%d" % h], ["X%d_0" % i])
+        act(zb[:, 0:768], T.X[:, x0:x0 + 768], ["X%d_0" % i], ["Z%d_0" % h], AF.Abs)
+        act(zb[:, 768:1024], xp, ["VP%d" % h], ["Z%d_r" % h], AF.Abs)
+        if h == 1:
+            dist(p, 1)
+        yield 400, 2300, 0
+
+    def first_dist(p):
+        if p not in issued:
+            issued.append(p)
+            dist(p, 0)
+
+    def dist(p, h):
+        zb = T["Z%d" % h]
+
+        def f():
             for k in range(16):
-                r_ = mm(key, T.WD[:, 15 - k:143 - k], zb[:, k::16], False, k == 15)
+                r_ = mm(bk[h][:, 128:192], T.WD[:, 15 - k:143 - k], zb[:, k::16], False, k == 15)
             return r_
-        op("t", f, ["IB", "PC1", "PC2%d" % i, "WD", "Z%d_0" % h, "Z%d_1" % h, "Z%d_r" % h], ["BK%d" % h])
+        op("t", f, ["WD", "Z%d_0" % h, "Z%d_r" % h], ["BK%d" % h])
 
     def names(p, h):
         i = p * 2 + h
@@ -523,28 +529,54 @@ def rank_program(g, core, T, topo):
 
     def best(p, h):
         i = p * 2 + h
+        first_dist(p)
         scan(T.KS[:, i * 64:i * 64 + 64], T.RB[:], bk[h][:, 128:192], OP.max, OP.min, ["RB", "BK%d" % h], ["KS%d" % i])
 
     def arg_gen(h, q):
         x = "%d" % h
         hh = slice(h * 64, h * 64 + 64)
         best(0, h)
-        yield
+        yield 60, 180, 0
         ki = T.KI[:, h * 8:h * 8 + 4]
         ka = T.KI[:, h * 8 + 4:h * 8 + 8]
         cp(ki, T.KS[:, h * 64 + 15:h * 64 + 64:16], ["KS" + x], ["KI" + x])
-        yield
+        yield 60, 180, 0
         ts(ka, ki, 1023, AND, ["KI" + x], ["KA_" + x])
-        yield
+        yield 60, 180, 0
         lp = T.LP[:, h * 8:h * 8 + 4]
         cp(lp, ka, ["KA_" + x], ["LP" + x])
-        yield
+        yield 60, 180, 0
         tt(T.CS[:, hh], T.X[:, h * 1024:h * 1024 + 1024].indirect(lp), T.E2M[:, hh], OP.add,
            ["X%s_0" % x, "X%s_r" % x, "LP" + x, "E2Ma" + x, "E2Mb" + x], ["CS" + x])
-        yield
+        yield 160, 180, 0
         ts(T.C2[:, hh], T.CS[:, hh], MAGIC, OP.add, ["CS" + x], ["C2" + x], MAGIC, OP.subtract)
         u_mm(q, h, T.C2[:, hh], "C2" + x)
-        yield
+        yield 60, 700, 0
+
+    def chain(h, q):
+        yield 0, 1100 * h, 0
+        for x in (e_gen(h, q), hash_gen(0, h, q), cand(0, h, q), arg_gen(h, q), hash_gen(1, h, q), cand(1, h, q)):
+            for y in x:
+                yield y
+        names(0, h)
+        yield 60, 0, 0
+        names(1, h)
+        yield 60, 2100, 0
+        best(1, h)
+        yield 60, 0, 0
+
+    def r_mm(b):
+        pk = T["PK%d" % b]
+        mm(pk[:], T.IH[:], T.RCA[:, b * 512:b * 512 + 512], True, False)
+        for c in range(4):
+            mm(pk[:, c * 128:c * 128 + 128], T.IH[:], T.A16[:], False, False)
+        return mm(pk[:], T.IH[:], T.RCB[:, b * 512:b * 512 + 512], False, False)
+
+    def ahead(q):
+        for b in range(2):
+            op("t", lambda: r_mm(b), ["IH", "A16"] + ["RC%s%d" % (x, c) for x in "AB" for c in range(8)], ["PK%d" % b])
+        ts(T.S0M[:], T.S2[:], T.NMX[:, q:q + 1], OP.mult, ["S2", "NMX"], ["S0M"], 767.0, OP.max)
+        yield 150, 0, 0
 
     for t in range(NR):
         q = (rank + 1 + t) % NR
@@ -552,30 +584,8 @@ def rank_program(g, core, T, topo):
             e_load(T.F0[:, 0:2064], f0)
         else:
             e_load(T.F[:], fall)
-        run(e_gen(0, q))
-        run(e_gen(1, q), hash_gen(0, 0, q))
-        cand(0, 0, q)
-        dist(0, 0)
-        run(hash_gen(0, 1, q))
-        cand(0, 1, q)
-        run(arg_gen(0, q))
-        for b in range(2):
-            op("t", lambda: mm(T["PK%d" % b][:], T.IH[:], T.RC[:, b * 512:b * 512 + 512], True, False), ["IH", "RC%d" % b], ["PK%d" % b])
-        dist(0, 1)
-        names(0, 0)
-        run(hash_gen(1, 0, q))
-        cand(1, 0, q)
-        run(arg_gen(1, q))
-        dist(1, 0)
-        names(0, 1)
-        run(hash_gen(1, 1, q))
-        cand(1, 1, q, 2)
-        dist(1, 1)
-        best(1, 0)
-        names(1, 0)
-        names(1, 1)
-        ts(T.S0M[:], T.S2[:], T.NMX[:, q:q + 1], OP.mult, ["S2", "NMX"], ["S0M"], 767.0, OP.max)
-        best(1, 1)
+        issued.clear()
+        run(chain(0, q), chain(1, q), ahead(q))
         kf, nf, ps, pm, kl, pia = (T.KFI[:, i * 8:i * 8 + 8] for i in range(6))
         tt(kf, T.KS[:, 15:128:16], T.KS[:, 143:256:16], OP.min, ["KS0", "KS1", "KS2", "KS3"], ["kf"])
         ts(nf, kf, T.THK[:, q:q + 1], OP.is_ge, ["kf", "THK"], ["nf"], 256.0, OP.mult)
@@ -610,7 +620,7 @@ def rank_program(g, core, T, topo):
                                             apply_absolute_value=True), ["PK%d" % (c // 4)], ["KB%d" % c])
             if c == 3 and t < NR - 1:
                 tt(T.F[:, q * 1024 + 512:q * 1024 + 640], T.X[:].indirect(T.LF[:]), T.E1[:], OP.add,
-                   ["X%d_%s" % (i, j) for i in range(4) for j in "01r"] + ["LF", "E10", "E11", "E1z"], ["FW%d" % q])
+                   ["X%d_%s" % (i, j) for i in range(4) for j in "0r"] + ["LF", "E10", "E11", "E1z"], ["FW%d" % q])
         tt(T.KBI[:], T.KB[:], T.NFT[:], OP.max, ["KB%d" % c for c in range(8)] + ["NFT"], ["KBI"])
         tt(T.KBX[:], T.KBI[:].indirect(T.REP[:]), T.DL[:], OP.mult, ["KBI", "REP", "DL"], ["KBX"])
         ts(pia, T.KBI[:], 127, AND, ["KBI"], ["pia"])
@@ -623,22 +633,22 @@ def rank_program(g, core, T, topo):
         tt(nq, T.NP1[:].indirect(T.LPI[:]), T.NP2[:], OP.not_equal, ["NP1", "NP2", "LPI"], ["nq"])
         tt(mnn, T.NP1[:].indirect(T.LPI[:]), T.NP2[:], OP.min, ["NP1", "NP2", "LPI"], ["mnn"])
         cp(sp, T.S1[:].indirect(T.LPI[:]), ["S1", "LPI"], ["sp"])
+        ts(am, T.KRS[:], 128.0, OP.is_ge, ["KRS", "VP0", "VP1"], ["am"])
         tt(cl, nq, mnn, OP.mult, ["nq", "mnn"], ["cl"])
-        ts(am, T.KRS[:], 128.0, OP.is_ge, ["KRS", "VP0"], ["am"])
+        tt(sa, sp, am, OP.mult, ["sp", "am"], ["sa"])
         tt(bm, T.KRP[:], T.C128[:], OP.is_equal, ["KRP", "C128"], ["bm"])
+        tt(m_, T.S1[:], sa, OP.max, ["S1", "sa"], ["m"])
         tt(ef, am, bm, OP.max, ["am", "bm"], ["ef"])
+        tt(ds, T.SDV[:], m_, OP.subtract, ["SDV", "m"], ["ds"])
         tt(T.CLE[:], cl, ef, OP.mult, ["cl", "ef"], ["CLE"])
         op("t", lambda: mm(T.KA[:, 128:256], T.BOB[:], T.CLE[:], True, True), ["BOB", "CLE"], ["KA"])
-        tt(sa, sp, am, OP.mult, ["sp", "am"], ["sa"])
-        ts(kep, T.CLE[:], 0.0, OP.is_equal, ["CLE", "VP1"], ["kep"])
-        tt(m_, T.S1[:], sa, OP.max, ["S1", "sa"], ["m"])
-        tt(k0, T.S1[:], kep, OP.mult, ["S1", "kep"], ["k0"])
-        tt(ds, T.SDV[:], m_, OP.subtract, ["SDV", "m"], ["ds"])
-        ts(k0, k0, 767.0, OP.max, ["k0"], ["k0"])
         tt(dsb, ds, bm, OP.mult, ["ds", "bm"], ["dsb"])
+        ts(kep, T.CLE[:], 0.0, OP.is_equal, ["CLE"], ["kep"])
         tt(alt, m_, dsb, OP.add, ["m", "dsb"], ["alt"])
-        tt(dd, alt, k0, OP.subtract, ["alt", "k0"], ["dd"])
+        tt(k0, T.S1[:], kep, OP.mult, ["S1", "kep"], ["k0"])
+        ts(k0, k0, 767.0, OP.max, ["k0"], ["k0"])
         ts(nan, T.KA[:, 128:256], 0.0, OP.is_equal, ["KA"], ["nan"])
+        tt(dd, alt, k0, OP.subtract, ["alt", "k0"], ["dd"])
         tt(dsb, dd, nan, OP.mult, ["dd", "nan"], ["dsb"])
         tt(T.S2[:], k0, dsb, OP.add, ["k0", "dsb", "VP0", "VP1"], ["S2"])
         if t < NR - 1:

from concourse.bass import DstId, RemoteDMATransfer
from concourse.mybir import AluOpType, AxisListType, ActivationFunctionType

OP = AluOpType
AF = ActivationFunctionType
NR, W = 8, 4096
MAGIC = 25165824.0

f32, b16, h16, i32, u16 = "float32", "bfloat16", "float16", "int32", "uint16"
SCRATCH = {}
for _d, _l in (
        (b16, "TZ 32768 F 8192 F0 2064 X 4096 Z0 1024 Z1 1024 VF 2048 VA 2048 MX 2048 MN 2048 EREP 2048 SB 4096 Y 4096 RM 1024 R255 1024 "
              "BOB 128 IB 128 IBN 128 WD 144 MK 64 PC1 64 PC2 256 W1L 1024 W2L 1024 C2 128 E20 64 E21 64 E1 128 CLE 128"),
        (h16, "TPH 256 PERM 512 NMO 256 NM 256 NMT 256 SW 272 HWO 4 HWN 64 BOH 128 BOK 128 IH 128 WS 144 RCA 1024 RCB 1024 CB 1024 "
              "A16 128 CW 128 KX 1024 HGD 128 HTS 128 KBX 128"),
        (i32, "TPI 128 SDI 128 HWI 3 THI 1 IP 16 IC 256 IC15 256 ICG 128 C48 64 L0T 128 S2 128 UI 16 UA 16 PP 8 VI 16 HI 128 HM 256 KI 16 "
              "KFI 64 S1 128 NP1 128 NP2 128 KBI 8"),
        (u16, "EL 64 REP 8 REP4 4 LL 256 LE 128 LH 256 LP 16 LN 8 LF 8 LPI 8"),
        (f32, "COL 32 DL 128 RU 128 RB 64 CWT 128 C128 128 CT 8 CTT 8 CBC 8 SG 128 NMX 8 W1F 8 W2F 8 KCF 8 THK 8 KC 1024 SDV 128 S0M 128 "
              "US 256 KK 128 HC 272 KS 256 CS 128 E2M 128 HIM 128 SUM 128 NFT 8 KB 8 KRS 128 KRP 128 PR 1024 YO 128")):
    _l = _l.split()
    for _i in range(0, len(_l), 2):
        SCRATCH[_l[_i]] = ("sbuf", [128, int(_l[_i + 1])], _d)
BANKS = ("BK0", "BK1", "PK0", "PK1", "HS", "KA", "VP0", "VP1")
for _n in BANKS:
    SCRATCH[_n] = ("psum", [128, 512], f32)
SEMAPHORES = ["v", "s", "t", "gp", "nm", "hn", "ft", "fs", "ls", "hz0", "hz1"] + ["d%d" % i for i in range(20)] + \
    ["ta%d" % q for q in range(NR)] + ["tb%d" % q for q in range(NR)]


def mask_of(engs):
    return sum(1 << e for e in engs)


def places(T, topo):
    chips, relay, used = [], {}, []
    for r, c in enumerate(T.cores):
        if not chips or topo.chip(T.cores[chips[-1][0]]) != topo.chip(c):
            chips.append([])
        chips[-1].append(r)
        relay[r] = [x for x in topo.cores_of(c) if x not in T.cores and x not in used and topo.die(x) != topo.die(c)
                    and all(topo.may_write(x, d) for d in T.cores)][0]
        used.append(relay[r])
    return chips, relay


def rank_program(g, core, T, topo):
    chips, relay = places(T, topo)
    ncl = len(chips)
    ls = [0]

    def targets(r):
        n = [i for i in range(ncl) if r in chips[i]][0]
        return [T.cores[chips[(n - 1 - d) % ncl][-1]] for d in range(ncl - 1)]

    def send(dst, lo, hi, sem, engs):
        rid, pid = topo.addr(dst)[:2]
        g.remote_dma(T.TZ[:, lo:hi], T.TZ[:, lo:hi], T.sem[sem], T.sem.ls, pid, rid, mask_of(engs))
        ls[0] += len(engs)

    rank = T.rank_of(core)
    H2, Q4 = W // 2, W // 4
    if rank is None:
        for r in range(NR):
            if relay[r] == core:
                for n, d in enumerate(targets(r)):
                    for i in range(2):
                        if n == 0:
                            g.wait_ge(T.sem["hz%d" % i], 8)
                        o = r * W + H2 + i * Q4
                        send(d, o, o + Q4, "tb%d" % r, topo.engines(core, d)[:8])
                g.wait_ge(T.sem.ls, ls[0])
        return

    Q = {"v": g.vector, "s": g.scalar, "t": g.tensor, "g": g, "y": g.sync}
    SEM = {"v": "v", "s": "s", "t": "t", "g": "gp"}
    cnt = {e: 0 for e in SEM}
    clk = {e: {} for e in Q}
    hist, lastw, readers, ndma = {}, {}, {}, [0]

    def wait(e, need):
        for s, n in sorted(need.items()):
            if clk[e].get(s, 0) < n:
                Q[e].wait_ge(T.sem[s], n)
                for s2, n2 in hist.get((s, n), {}).items():
                    clk[e][s2] = max(clk[e].get(s2, 0), n2)
                clk[e][s] = max(clk[e].get(s, 0), n)

    def deps(e, R, Wt):
        toks = [k for tg in R for k in lastw.get(tg, ())]
        toks += [k for tg in R if tg in BANKS for k in readers.get(tg, {}).items() if k[0] != SEM.get(e)]
        toks += [k for tg in Wt for k in lastw.get(tg, ()) if not (e == "t" and k[0] == "t")]
        toks += [k for tg in Wt for k in readers.get(tg, {}).items() if k[0] != SEM.get(e)]
        need = {}
        for s, n in toks:
            need[s] = max(need.get(s, 0), n)
        return need

    def done(tok, R, Wt):
        for tg in R:
            readers.setdefault(tg, {})[tok[0]] = tok[1]
        for tg in Wt:
            lastw[tg] = [tok]
            readers[tg] = {}

    def op(e, fn, R, Wt):
        wait(e, deps(e, R, Wt))
        ins = fn()
        for i in (ins if isinstance(ins, list) else [ins]):
            i.then_inc(T.sem[SEM[e]], 1)
            cnt[e] += 1
            hist[(SEM[e], cnt[e])] = dict(clk[e])
        done((SEM[e], cnt[e]), R, Wt)

    def dma(e, out, in_, R, Wt):
        wait(e, deps(e, R, Wt))
        s = "d%d" % ndma[0]
        ndma[0] += 1
        Q[e].dma_start(out, in_).then_inc(T.sem[s], 16)
        hist[(s, 16)] = dict(clk[e])
        done((s, 16), R, Wt)

    V, S, PE = g.vector, g.scalar, g.tensor
    mm = PE.matmul

    def ts(out, a, s1, o1, R, Wt, s2=None, o2=None):
        if o2 is None:
            op("v", lambda: V.tensor_scalar(out, a, s1, None, o1), R, Wt)
        else:
            op("v", lambda: V.tensor_scalar(out, a, s1, s2, o1, o2), R, Wt)

    def tt(out, a, b, o, R, Wt):
        op("v", lambda: V.tensor_tensor(out, a, b, o), R, Wt)

    def cp(out, a, R, Wt):
        op("v", lambda: V.tensor_copy(out, a), R, Wt)

    def fill(ap, x, Wt):
        op("v", lambda: V.memset(ap, x), [], Wt)

    def scan(out, d0, d1, o0, o1, R, Wt):
        op("v", lambda: V.tensor_tensor_scan(out, d0, d1, 0.0, o0, o1), R, Wt)

    def act(out, a, R, Wt, func=AF.Copy, bias=0.0, scale=1.0):
        op("s", lambda: S.activation(out, a, func, bias=bias, scale=scale), R, Wt)

    z0 = rank * W
    dma("y", T.TPI[:], T.tp[:], [], ["TPI"])
    dma("s", T.SDI[:], T.sd[:], [], ["SDI"])
    dma("y", T.HWI[:], T.hw[:], [], ["HWI"])
    dma("s", T.THI[:], T.th[:], [], ["THI"])
    dma("y", T.TZ[:, z0:z0 + H2], T.tz[:, 0:H2], [], ["TZa%d" % rank])
    dma("s", T.TZ[:, z0 + H2:z0 + W], T.tz[:, H2:W], [], ["TZb%d" % rank])
    op("g", lambda: g.iota(T.IP[:, 0:1], [[0, 1]], 0, 1), [], ["IP"])
    op("g", lambda: g.iota(T.IC[:], [[1, 256]], 0, 0), [], ["IC"])

    C = {}
    ip = {"P": T.IP[:, 0:1]}

    def icol(name, *a):
        n = len(ip)
        ip[name] = T.IP[:, n:n + 1]
        ts(ip[name], ip["P"], a[0], a[1], ["IP"], ["i" + name], *a[2:])

    def col(name, src, s1, o1, s2=None, o2=None, R=()):
        i = len(C)
        C[name] = T.COL[:, i:i + 1]
        ts(C[name], src, s1, o1, ["IP"] + ["i" + x for x in ip] + list(R), ["c" + name], s2, o2)

    AND, SHR = OP.bitwise_and, OP.arith_shift_right
    icol("K", 15, AND)
    icol("Q", 14, AND)
    icol("S", 1, AND)
    icol("G", 4, SHR)
    icol("B3", 3, SHR, 1, AND)
    icol("B4", 4, SHR, 1, AND)
    icol("B5", 5, SHR)
    icol("L", 7, AND)
    col("S8", ip["S"], 8.0, OP.mult)
    col("G8", ip["G"], 1.0, OP.mult)
    col("PM0", ip["Q"], 16.0, OP.mult, C["S8"], OP.add, ["cS8"])
    col("PM", C["PM0"], C["G8"], OP.add, None, None, ["cPM0", "cG8"])
    col("P", ip["P"], 1.0, OP.mult)
    ts(T.PERM[:, 0:256], T.IC[:], C["PM"], OP.is_equal, ["IC", "cPM"], ["PERM0"])
    ts(T.PERM[:, 256:512], T.IC[:], -16.0, OP.add, ["IC", "cPM"], ["PERM1"], C["PM"], OP.is_equal)
    ts(T.IH[:], T.IC[:, 0:128], C["P"], OP.is_equal, ["IC", "cP"], ["IH"])
    ts(T.TPH[:, 0:128], T.TPI[:], -2047.0, OP.add, ["TPI"], ["TPH0"])
    ts(T.TPH[:, 128:256], T.SDI[:], -2047.0, OP.add, ["SDI"], ["TPH1"])

    def turn():
        mm(T.HS[:, 0:256], T.TPH[:, 0:128], T.PERM[:, 0:256], True, False)
        return mm(T.HS[:, 0:256], T.TPH[:, 128:256], T.PERM[:, 256:512], False, True)
    op("t", turn, ["TPH0", "TPH1", "PERM0", "PERM1"], ["HS"])
    cp(T.HWO[:, 0:3], T.HWI[:], ["HWI"], ["HWO0"])
    ts(T.HWO[:, 3:4], T.THI[:], -2048.0, OP.add, ["THI"], ["HWO1"])
    cp(T.NMO[:], T.HS[:, 0:256], ["HS"], ["NMO"])
    cp(T.NM[:, rank * 32:rank * 32 + 32], T.NMO[:, rank * 32:rank * 32 + 32], ["NMO"], ["NMo"])
    cp(T.HWN[:, rank * 8:rank * 8 + 4], T.HWO[:], ["HWO0", "HWO1"], ["HWo"])

    mine = [c for c in chips if rank in c][0]
    far = [r for r in range(NR) if r not in mine]
    near = [r for r in mine if r != rank][0]
    others = far + [near]
    last = rank == mine[-1]
    fe = topo.engines(core, T.cores[far[0]])
    ne = [e for e in topo.engines(core, T.cores[near]) if e not in fe]
    slots = fe[:6] + [fe[6]] if last else fe[4:] + fe[4:6] + [ne[0]]

    def did(r):
        a = topo.addr(T.cores[r])
        return DstId(rid=a[0], pnc=a[1])

    def spread(src, dst, sem, engs):
        todo = [(r, e) for r, e in zip(others, engs)]
        while todo:
            tr, seen, rest = [], [], []
            for r, e in todo:
                if e in seen:
                    rest.append((r, e))
                else:
                    seen.append(e)
                    tr.append(RemoteDMATransfer(dst_ids=[did(r)], dma_engine_mask=1 << e, remote_sem=T.sem[sem], srcs=[src(r)], dsts=[dst]))
            g.remote_dma_fused(tr, local_sem=T.sem.ls)
            ls[0] += len(tr)
            todo = rest

    wait("g", deps("g", ["NMO"], []))
    spread(lambda r: T.NMO[:, r * 32:r * 32 + 32], T.NM[:, rank * 32:rank * 32 + 32], "nm", fe)
    wait("g", deps("g", ["HWO0", "HWO1"], []))
    g.remote_dma_fused([RemoteDMATransfer(dst_ids=[did(r) for r in others], dma_engine_mask=1 << fe[7], remote_sem=T.sem.hn, srcs=[T.HWO[:]],
                                          dsts=[T.HWN[:, rank * 8:rank * 8 + 4] for _ in others])], local_sem=T.sem.ls)
    ls[0] += 1
    lastw["NM"], lastw["HWN"] = [("nm", 7)], [("hn", 7)]

    def direct(d, engs):
        wait("g", deps("g", ["TZa%d" % rank], []))
        for i in range(8 // len(engs)):
            n = H2 * len(engs) // 8
            send(d, z0 + i * n, z0 + i * n + n, "ta%d" % rank, engs)

    def to_relay():
        wait("g", deps("g", ["TZb%d" % rank], []))
        for i in range(2):
            send(relay[rank], z0 + H2 + i * Q4, z0 + H2 + (i + 1) * Q4, "hz%d" % i, ne[:8])

    def hand_on(q):
        for h, x in enumerate("ab"):
            wait("g", deps("g", ["TZ%s%d" % (x, q)], []))
            send(T.cores[near], q * W + h * H2, q * W + (h + 1) * H2, "t%s%d" % (x, q), ne)

    if last:
        hand_on(rank)
    else:
        direct(targets(rank)[0], fe[:4])
        to_relay()
    ntb = {q: 16 if last and q in far else 8 for q in range(NR)}
    for q in range(NR):
        if q != rank:
            lastw["TZa%d" % q] = [("ta%d" % q, 8)]
            lastw["TZb%d" % q] = [("tb%d" % q, ntb[q])]

    col("K", ip["K"], 1.0, OP.mult)
    col("PG", ip["G"], 16.0, OP.mult)
    col("PGF", C["PG"], 15.0, OP.add, None, None, ["cPG"])
    col("QB", ip["Q"], 512.0, OP.mult)
    col("S128", ip["S"], 128.0, OP.mult)
    col("E0", ip["K"], 0.0, OP.is_equal)
    col("E1", ip["K"], 1.0, OP.is_equal, 2048.0, OP.mult)
    col("J128", ip["K"], 128.0, OP.mult)
    col("B3", ip["B3"], 8.0, OP.add)
    col("R2", ip["B5"], 2.0, OP.mult, C["B3"], OP.add, ["cB3"])
    col("SW", ip["L"], 16.0, OP.mult, C["R2"], OP.add, ["cR2"])
    col("T1", ip["B4"], 1.0, OP.mult)
    col("T0", ip["B4"], 0.0, OP.is_equal)
    ic = T.IC[:, 0:128]
    for ty in range(2):
        ts(T.SW[:, ty * 136:ty * 136 + 136], T.IC[:, 0:136], C["SW"], OP.is_equal, ["IC", "cSW", "cT%d" % ty], ["SW%d" % ty], C["T%d" % ty], OP.mult)
    fill(T.F0[:, 2048:2064], -256.0, ["F0e"])
    ts(T.L0T[:], ic, C["J128"], OP.add, ["IC", "cJ128"], ["L0T"])
    pr = [T.PR[:, i * 128:i * 128 + 128] for i in range(8)]
    ts(pr[0], T.TPI[:], 0.0, OP.is_lt, ["TPI"], ["pr0"], 2048.0, OP.mult)
    tt(pr[1], T.L0T[:], pr[0], OP.max, ["L0T", "pr0"], ["pr1"])
    cp(T.LE[:], pr[1], ["pr1"], ["LE"])
    for b, (x, y) in enumerate(((0.0, 1.0), (255.0, 0.0))):
        rm = (T.RM, T.R255)[b]
        fill(rm[:], y, ["RM%d" % b])
        fill(rm[:, 0::16], x, ["RM%d" % b])
    fill(T.RU[:], 0.0, ["RU"])
    fill(T.RU[:, 0::16], -1e9, ["RU"])
    fill(T.RB[:], 0.0, ["RB"])
    fill(T.RB[:, 0::16], 1e9, ["RB"])
    op("t", lambda: [mm(T.HS[:, b * 128:b * 128 + 128], T.NM[:, b * 128:b * 128 + 128], T.IH[:], True, True) for b in range(2)],
       ["NM", "NMo", "IH"], ["HS"])
    cp(T.NMT[:], T.HS[:, 0:256], ["HS"], ["NMT"])

    def back():
        out = []
        for ty in range(2):
            o = T.KA[:, ty * 128:ty * 128 + 128]
            mm(o, T.SW[:, ty * 136 + 8:ty * 136 + 136], T.NMT[:, 0:128], True, False)
            out.append(mm(o, T.SW[:, ty * 136:ty * 136 + 128], T.NMT[:, 128:256], False, True))
        return out
    op("t", back, ["SW0", "SW1", "NMT"], ["KA"])
    ts(T.LL[:], T.KA[:, 0:256], 2047.0, OP.add, ["KA"], ["LL"], 0.0, OP.max)
    tzo = ["TZa%d" % rank, "TZb%d" % rank]

    def feats(ty):
        y0 = ty * 2048
        win = T.TZ[:, z0:z0 + W]
        act(T.Y[:, y0:y0 + 1024], win.indirect(T.LL[:, ty * 128:ty * 128 + 64]), tzo + ["LL"], ["Ya%d" % ty])
        cp(T.Y[:, y0 + 1024:y0 + 2048], win.indirect(T.LL[:, ty * 128 + 64:ty * 128 + 128]), tzo + ["LL"], ["Yb%d" % ty])
        for r in others + [rank]:
            for s in range(2):
                src = T.Y[:, y0 + 2 * r + s:y0 + 2048:16]
                o = r * 512 + ty * 256 + s * 128
                out, tag = T.SB[:, o:o + 128], "SB%d_%d_%d" % (r, ty, s)
                if r == rank and ty == 0:
                    out, tag = T.F0[:, rank * 256 + s * 128:rank * 256 + s * 128 + 128], "F0o%d" % s
                elif r == rank:
                    o = rank * 1024 + 256 + s * 128
                    out, tag = T.F[:, o:o + 128], "Fso%d" % s
                (cp if s == 0 else act)(out, src, ["Ya%d" % ty, "Yb%d" % ty], [tag])
        wait("g", deps("g", ["SB%d_%d_%d" % (r, ty, s) for r in others for s in range(2)], []))
        d = T.F0[:, rank * 256:rank * 256 + 256] if ty == 0 else T.F[:, rank * 1024 + 256:rank * 1024 + 512]
        spread(lambda r: T.SB[:, r * 512 + ty * 256:r * 512 + ty * 256 + 256], d, "fs" if ty else "ft", slots)
        lastw["Fsr" if ty else "F0r"] = [("fs" if ty else "ft", 7)]

    feats(0)
    feats(1)
    f0 = ["F0r", "F0o0", "F0o1", "F0e"]
    if last:
        direct(targets(rank)[0], fe)
        to_relay()
    for d in targets(rank)[1:]:
        direct(d, fe)
    if not last:
        hand_on(rank)
    else:
        n = [i for i in range(ncl) if rank in chips[i]][0]
        for d in range(1, ncl):
            for q in chips[(n + d) % ncl]:
                hand_on(q)

    ts(T.IC15[:], T.IC[:], 15, AND, ["IC"], ["IC15"])
    ts(T.ICG[:], ic, 112, AND, ["IC"], ["ICG"])
    ts(T.C48[:], T.IC[:, 0:64], 48, AND, ["IC"], ["C48"])
    ts(T.EL[:], T.C48[:], C["K"], OP.add, ["C48", "cK"], ["EL"])
    ts(T.MK[:], T.IC15[:, 0:64], C["K"], OP.not_equal, ["IC15", "cK"], ["MK"], -4194304.0, OP.mult)
    ts(T.IB[:], ic, C["P"], OP.is_equal, ["IC", "cP"], ["IB"])
    ts(T.IBN[:], ic, C["P"], OP.is_equal, ["IC", "cP"], ["IBN"], -1.0, OP.mult)
    ts(T.DL[:], T.IC15[:, 0:128], C["K"], OP.is_equal, ["IC15", "cK"], ["DL"])
    ts(T.BOB[:], T.ICG[:], C["PG"], OP.is_equal, ["ICG", "cPG"], ["BOB"])
    ts(T.BOH[:], T.ICG[:], C["PG"], OP.is_equal, ["ICG", "cPG"], ["BOH"])
    ts(T.BOK[:], T.ICG[:], C["PG"], OP.is_equal, ["ICG", "cPG"], ["BOK"], 1024.0, OP.mult)
    cp(T.REP[:], T.IC[:, 0:8], ["IC"], ["REP"])
    cp(T.REP4[:], T.IC[:, 4:8], ["IC"], ["REP4"])
    ts(T.WD[:], T.IC[:, 0:144], C["PGF"], OP.is_equal, ["IC", "cPGF"], ["WD"], 4096.0, OP.mult)
    ts(T.WS[:], T.IC[:, 0:144], C["PGF"], OP.is_equal, ["IC", "cPGF"], ["WS"], 1024.0, OP.mult)
    ts(T.PC1[:], T.IC15[:, 0:64], 16.0, OP.mult, ["IC15", "cK"], ["PC1"], C["K"], OP.add)
    for i in range(4):
        ts(T.PC2[:, i * 64:i * 64 + 64], T.C48[:], 16.0, OP.mult, ["C48"], ["PC2%d" % i], 1024.0 * i, OP.add)
    hwn = ["HWN", "HWo"]
    for i, x in enumerate((T.W1F, T.W2F, T.KCF)):
        cp(x[:], T.HWN[:, i::8], hwn, ["hw%d" % i])
    ts(T.THK[:], T.HWN[:, 3::8], 2048.0, OP.add, hwn, ["THK"], 4096.0, OP.mult)

    def hash_consts(q):
        o = slice(q * 128, q * 128 + 128)
        ts(T.W1L[:, o], T.BOB[:], T.W1F[:, q:q + 1], OP.mult, ["BOB", "hw0"], ["W1L%d" % q], 0.5, OP.mult)
        ts(T.W2L[:, o], T.BOB[:], T.W2F[:, q:q + 1], OP.mult, ["BOB", "hw1"], ["W2L%d" % q], 0.5, OP.mult)
        ts(T.KX[:, o], T.DL[:], T.KCF[:, q:q + 1], OP.mult, ["DL", "hw2"], ["KX%d" % q])
        op("t", lambda: mm(T.KA[:, 256:384], T.BOH[:], T.KX[:, o], True, True), ["BOH", "KX%d" % q], ["KA"])
        act(T.KC[:, o], T.KA[:, 256:384], ["KA"], ["KC%d" % q])

    for t in range(NR):
        hash_consts((rank + 1 + t) % NR)
    for q in range(NR):
        fill(T.F[:, q * 1024 + 512:(q + 1) * 1024], -256.0, ["FW%d" % q])
    for h in range(2):
        fill(T.E1[:, h * 64 + 48:h * 64 + 64], 0.0, ["E1z"])
    ts(T.CWT[:], ic, 512.0, OP.add, ["IC"], ["CWT"], 1.0 / 1024, OP.mult)
    ts(T.CW[:], T.CWT[:], C["E0"], OP.mult, ["CWT", "cE0", "cE1"], ["CW"], C["E1"], OP.add)
    ts(T.C128[:], ic, 128.0, OP.add, ["IC"], ["C128"])
    ts(T.CTT[:], T.IC[:, 0:8], 16.0, OP.mult, ["IC", "cK"], ["CTT"], C["K"], OP.add)
    ts(T.CT[:], T.CTT[:], 256.0, OP.add, ["CTT"], ["CT"], 1.0 / 256, OP.mult)
    ts(T.SG[:], ic, C["S128"], OP.add, ["IC", "cS128"], ["SG"])
    ts(T.NMX[:], T.IC[:, 0:8], 2.0, OP.mult, ["IC", "cK"], ["NMX"], C["K"], OP.not_equal)
    fill(T.HC[:, 256:272], -2048.0, ["HCe"])
    for src, add, out, tag in ((T.TPI, 0.0, T.S2, "S2"), (T.SDI, 256.0, T.SDV, "SDV")):
        ts(pr[2], src[:], 1.0, OP.add, ["TPI", "SDI"], ["pr2"], 1024.0, OP.mult)
        tt(pr[3], pr[2], T.SG[:], OP.add, ["pr2", "SG"], ["pr3"])
        ts(out[:], pr[3], add, OP.add, ["pr3"], [tag], 767.0, OP.max)
    cp(T.A16[:], ic, ["IC"], ["A16"])
    ts(T.CBC[:], T.IC[:, 0:8], C["G8"], OP.is_equal, ["IC", "cG8"], ["CBC"], -1024.0, OP.mult)
    for c in range(8):
        o = slice(c * 128, c * 128 + 128)
        ts(T.RCA[:, o], ic, T.CTT[:, c:c + 1], OP.is_ge, ["IC", "CTT"], ["RCA%d" % c], 128.0, OP.mult)
        ts(T.RCB[:, o], ic, T.CTT[:, c:c + 1], OP.is_equal, ["IC", "CTT"], ["RCB%d" % c], 128.0, OP.mult)
        ts(T.CB[:, o], T.A16[:], 0.0, OP.mult, ["A16", "CBC"], ["CB%d_%d" % (c // 4, c % 4)], T.CBC[:, c:c + 1], OP.add)
    for q in range(NR):
        dma("y", T.F[:, q * 1024:q * 1024 + 256], T.F0[:, q * 256:q * 256 + 256], f0, ["Ft%d" % q])
    fall = ["Ft%d" % q for q in range(NR)] + ["FW%d" % q for q in range(NR)] + ["Fsr", "Fso0", "Fso1"]

    def run(*gens):
        now, ready, rk = 0, [0] * len(gens), [0] * len(gens)
        live = list(range(len(gens)))
        while live:
            i = min(live, key=lambda j: (max(ready[j], now), rk[j], j))
            try:
                cost, lat, rk[i] = next(gens[i])
            except StopIteration:
                live.remove(i)
                continue
            now = max(now, ready[i]) + cost
            ready[i] = now + lat

    bk = [T.BK0, T.BK1]

    def u_mm(q, h, src, tag):
        o = slice(q * 128, q * 128 + 128)

        def f():
            out = []
            for u, wl in enumerate((T.W1L, T.W2L)):
                mm(bk[h][:, u * 64:u * 64 + 64], T.IB[:], T.MK[:], True, False)
                out.append(mm(bk[h][:, u * 64:u * 64 + 64], wl[:, o], src, False, True))
            return out
        op("t", f, ["IB", "MK", "W1L%d" % q, "W2L%d" % q, tag], ["BK%d" % h])

    def e_load(win, R):
        for h in range(2):
            o, l = h * 1024, h * 64
            act(T.VF[:, o:o + 512], win.indirect(T.LE[:, l:l + 32]), R + ["LE"], ["VFa%d" % h])
            cp(T.VF[:, o + 512:o + 1024], win.indirect(T.LE[:, l + 32:l + 64]), R + ["LE"], ["VFb%d" % h])
            act(T.VA[:, o:o + 1024], T.VF[:, o:o + 1024], ["VFa%d" % h, "VFb%d" % h], ["VA%d" % h], AF.Abs)

    def e_gen(h, q):
        o = slice(h * 1024, h * 1024 + 1024)
        hh = slice(h * 64, h * 64 + 64)
        end = slice(h * 1024 + 15, h * 1024 + 1024, 16)
        scan(T.MX[:, o], T.RM[:], T.VF[:, o], OP.mult, OP.max, ["RM0", "VFa%d" % h, "VFb%d" % h], ["MX%d" % h])
        yield 500, 400, 0
        ts(T.HIM[:, hh], T.MX[:, end], -0.5, OP.add, ["MX%d" % h], ["HIM%d" % h])
        scan(T.MN[:, o], T.R255[:], T.VA[:, o], OP.max, OP.min, ["RM1", "VA%d" % h], ["MN%d" % h])
        yield 500, 180, 0
        tt(T.SUM[:, hh], T.HIM[:, hh], T.MN[:, end], OP.add, ["HIM%d" % h, "MN%d" % h], ["SUM%d" % h])
        yield 120, 180, 0
        e2 = T["E2%d" % h]
        tg = "E2%d" % h
        ts(e2[:], T.SUM[:, hh], MAGIC, OP.add, ["SUM%d" % h], [tg], MAGIC, OP.subtract)
        u_mm(q, h, e2[:], tg)
        act(T.EREP[:, o], e2[:].indirect(T.EL[:]), [tg, "EL"], ["EREP%d" % h], scale=0.5)
        b = h * 64
        act(T.E2M[:, b:b + 48], e2[:, 0:48], [tg], ["E2Ma%d" % h], AF.Identity, bias=-0.5)
        act(T.E2M[:, b + 48:b + 64], e2[:, 48:64], [tg], ["E2Mb%d" % h], AF.Identity, bias=-0.5, scale=0.5)
        act(T.E1[:, b:b + 48], e2[:, 0:48], [tg, "E1z"], ["E1%d" % h], scale=0.5)
        yield 60, 700, 0

    def hash_gen(p, h, q):
        x = "%d" % h
        i = p * 2 + h
        us, kk, hi = T.US[:, h * 128:h * 128 + 128], T.KK[:, h * 64:h * 64 + 64], T.HI[:, h * 64:h * 64 + 64]
        ui, ua, pp, vi = T.UI[:, h * 8:h * 8 + 8], T.UA[:, h * 8:h * 8 + 8], T.PP[:, h * 4:h * 4 + 4], T.VI[:, h * 8:h * 8 + 4]
        scan(us, T.RU[:], bk[h][:, 0:128], OP.add, OP.max, ["RU", "BK" + x], ["US" + x])
        yield 120, 180, 0
        cp(ui, T.US[:, h * 128 + 15:h * 128 + 128:16], ["US" + x], ["UI" + x])
        yield 60, 180, 0
        ts(ua, ui, 4095, AND, ["UI" + x], ["UA" + x])
        yield 60, 180, 0
        tt(pp, T.UA[:, h * 8:h * 8 + 4], T.UA[:, h * 8 + 4:h * 8 + 8], OP.mult, ["UA" + x], ["PP" + x])
        tt(kk, ua.indirect(T.REP4[:]), T.KC[:, q * 128:q * 128 + 64], OP.mult, ["UA" + x, "REP4", "KC%d" % q], ["KK" + x])
        yield 230, 120, 0
        ts(vi, pp, 5, SHR, ["PP" + x], ["VI" + x])
        yield 60, 180, 0
        tt(hi, vi.indirect(T.REP[:, 0:4]), kk, OP.add, ["VI" + x, "KK" + x, "REP"], ["HI" + x])
        yield 150, 180, 0
        hm = T.HM[:, i * 64:i * 64 + 64]
        ts(hm, hi, 4095, AND, ["HI" + x], ["HM%d" % i])
        yield 60, 180, 0
        cp(T.LH[:, i * 64:i * 64 + 64], hm, ["HM%d" % i], ["LH%d" % i])
        yield 60, 180, 1

    issued = []

    def cand(p, h, q):
        i = p * 2 + h
        x0, l0, e0 = i * 1024, i * 64, h * 1024
        tz = T.TZ[:, q * W:q * W + W]
        R = ["TZa%d" % q, "TZb%d" % q, "LH%d" % i]
        zb, xp = T["Z%d" % h], T["VP%d" % h][:, 0:256]
        act(T.X[:, x0 + 768:x0 + 1024], tz.indirect(T.LH[:, l0 + 48:l0 + 64]), R, ["X%d_r" % i])

        def f():
            mm(xp, T.IB[:], T.X[:, x0 + 768:x0 + 1024], True, False)
            return mm(xp, T.IBN[:], T.EREP[:, e0 + 768:e0 + 1024], False, True)
        op("t", f, ["IB", "IBN", "X%d_r" % i, "EREP%d" % h], ["VP%d" % h])
        key = bk[h][:, 128:192]

        def keys():
            mm(key, T.IB[:], T.PC1[:], True, False)
            return mm(key, T.IB[:], T.PC2[:, i * 64:i * 64 + 64], False, False)
        op("t", keys, ["IB", "PC1", "PC2%d" % i], ["BK%d" % h])
        if h == 1:
            first_dist(p)
        tt(T.X[:, x0:x0 + 768], tz.indirect(T.LH[:, l0:l0 + 48]), T.EREP[:, e0:e0 + 768], OP.subtract, R + ["EREP%d" % h], ["X%d_0" % i])
        act(zb[:, 0:768], T.X[:, x0:x0 + 768], ["X%d_0" % i], ["Z%d_0" % h], AF.Abs)
        act(zb[:, 768:1024], xp, ["VP%d" % h], ["Z%d_r" % h], AF.Abs)
        if h == 1:
            dist(p, 1)
        yield 400, 2300, 0

    def first_dist(p):
        if p not in issued:
            issued.append(p)
            dist(p, 0)

    def dist(p, h):
        zb = T["Z%d" % h]

        def f():
            for k in range(16):
                r_ = mm(bk[h][:, 128:192], T.WD[:, 15 - k:143 - k], zb[:, k::16], False, k == 15)
            return r_
        op("t", f, ["WD", "Z%d_0" % h, "Z%d_r" % h], ["BK%d" % h])

    def names(p, h):
        i = p * 2 + h
        ts(T.HC[:, i * 64:i * 64 + 64], T.HM[:, i * 64:i * 64 + 64], -2047.0, OP.add, ["HM%d" % i], ["HC%d" % i])

    def best(p, h):
        i = p * 2 + h
        first_dist(p)
        scan(T.KS[:, i * 64:i * 64 + 64], T.RB[:], bk[h][:, 128:192], OP.max, OP.min, ["RB", "BK%d" % h], ["KS%d" % i])

    def arg_gen(h, q):
        x = "%d" % h
        hh = slice(h * 64, h * 64 + 64)
        best(0, h)
        yield 60, 180, 0
        ki = T.KI[:, h * 8:h * 8 + 4]
        ka = T.KI[:, h * 8 + 4:h * 8 + 8]
        cp(ki, T.KS[:, h * 64 + 15:h * 64 + 64:16], ["KS" + x], ["KI" + x])
        yield 60, 180, 0
        ts(ka, ki, 1023, AND, ["KI" + x], ["KA_" + x])
        yield 60, 180, 0
        lp = T.LP[:, h * 8:h * 8 + 4]
        cp(lp, ka, ["KA_" + x], ["LP" + x])
        yield 60, 180, 0
        tt(T.CS[:, hh], T.X[:, h * 1024:h * 1024 + 1024].indirect(lp), T.E2M[:, hh], OP.add,
           ["X%s_0" % x, "X%s_r" % x, "LP" + x, "E2Ma" + x, "E2Mb" + x], ["CS" + x])
        yield 160, 180, 0
        ts(T.C2[:, hh], T.CS[:, hh], MAGIC, OP.add, ["CS" + x], ["C2" + x], MAGIC, OP.subtract)
        u_mm(q, h, T.C2[:, hh], "C2" + x)
        yield 60, 700, 0

    def chain(h, q):
        yield 0, 1100 * h, 0
        for x in (e_gen(h, q), hash_gen(0, h, q), cand(0, h, q), arg_gen(h, q), hash_gen(1, h, q), cand(1, h, q)):
            for y in x:
                yield y
        names(0, h)
        yield 60, 0, 0
        names(1, h)
        yield 60, 2100, 0
        best(1, h)
        yield 60, 0, 0

    def r_mm(b):
        pk = T["PK%d" % b]
        mm(pk[:], T.IH[:], T.RCA[:, b * 512:b * 512 + 512], True, False)
        for c in range(4):
            mm(pk[:, c * 128:c * 128 + 128], T.IH[:], T.A16[:], False, False)
        return mm(pk[:], T.IH[:], T.RCB[:, b * 512:b * 512 + 512], False, False)

    def ahead(q):
        for b in range(2):
            op("t", lambda: r_mm(b), ["IH", "A16"] + ["RC%s%d" % (x, c) for x in "AB" for c in range(8)], ["PK%d" % b])
        ts(T.S0M[:], T.S2[:], T.NMX[:, q:q + 1], OP.mult, ["S2", "NMX"], ["S0M"], 767.0, OP.max)
        yield 150, 0, 0

    for t in range(NR):
        q = (rank + 1 + t) % NR
        if t == 0:
            e_load(T.F0[:, 0:2064], f0)
        else:
            e_load(T.F[:], fall)
        issued.clear()
        run(chain(0, q), chain(1, q), ahead(q))
        kf, nf, ps, pm, kl, pia = (T.KFI[:, i * 8:i * 8 + 8] for i in range(6))
        tt(kf, T.KS[:, 15:128:16], T.KS[:, 143:256:16], OP.min, ["KS0", "KS1", "KS2", "KS3"], ["kf"])
        ts(nf, kf, T.THK[:, q:q + 1], OP.is_ge, ["kf", "THK"], ["nf"], 256.0, OP.mult)
        ts(ps, kf, 4095, AND, ["kf"], ["ps"], 4, SHR)
        tt(pm, nf, ps, OP.max, ["nf", "ps"], ["pm"])
        cp(T.LN[:], pm, ["pm"], ["LN"])
        tt(T.HGD[:], T.HC[:].indirect(T.LN[:]), T.DL[:], OP.mult, ["HC0", "HC1", "HC2", "HC3", "HCe", "LN", "DL"], ["HGD"])
        op("t", lambda: mm(T.HS[:, 0:128], T.HGD[:], T.IH[:], True, True), ["HGD", "IH"], ["HS"])

        def sv():
            wl = T.WS[:, 15 - 2 * q:143 - 2 * q]
            mm(T.HS[:, 128:256], wl, T.CW[:], True, False)
            return mm(T.HS[:, 128:256], wl, T.HGD[:], False, True)
        op("t", sv, ["WS", "CW", "HGD"], ["HS"])
        for b in range(2):
            pk = T["PK%d" % b]
            op("t", lambda: [mm(pk[:, c * 128:c * 128 + 128], T.BOK[:], T.HGD[:], False, False) for c in range(4)][-1],
               ["BOK", "HGD"], ["PK%d" % b])
            if b == 0:
                cp(T.HTS[:], T.HS[:, 0:128], ["HS"], ["HTS"])
            op("t", lambda: mm(pk[:], T.HTS[:], T.CB[:, b * 512:b * 512 + 512], False, True),
               ["HTS"] + ["CB%d_%d" % (b, c) for c in range(4)], ["PK%d" % b])
        tt(T.S1[:], T.HS[:, 128:256], T.S0M[:], OP.max, ["HS", "S0M"], ["S1"])
        tt(T.NFT[:], nf, T.CT[:], OP.mult, ["nf", "CT"], ["NFT"])
        ts(kl, kf, 4095, AND, ["kf"], ["kl"])
        ts(T.NP1[:], T.S1[:], 10, SHR, ["S1"], ["NP1"])
        cp(T.LF[:], kl, ["kl"], ["LF"])
        ts(T.NP2[:], T.S1[:], 10, SHR, ["S1"], ["NP2"])
        for c in range(8):
            pk = T["PK%d" % (c // 4)]
            op("v", lambda: V.tensor_reduce(T.KB[:, c:c + 1], pk[:, (c % 4) * 128:(c % 4) * 128 + 128], AxisListType.X, OP.min,
                                            apply_absolute_value=True), ["PK%d" % (c // 4)], ["KB%d" % c])
            if c == 3 and t < NR - 1:
                tt(T.F[:, q * 1024 + 512:q * 1024 + 640], T.X[:].indirect(T.LF[:]), T.E1[:], OP.add,
                   ["X%d_%s" % (i, j) for i in range(4) for j in "0r"] + ["LF", "E10", "E11", "E1z"], ["FW%d" % q])
        tt(T.KBI[:], T.KB[:], T.NFT[:], OP.max, ["KB%d" % c for c in range(8)] + ["NFT"], ["KBI"])
        tt(T.KBX[:], T.KBI[:].indirect(T.REP[:]), T.DL[:], OP.mult, ["KBI", "REP", "DL"], ["KBX"])
        ts(pia, T.KBI[:], 127, AND, ["KBI"], ["pia"])
        op("t", lambda: mm(T.KA[:, 0:128], T.BOH[:], T.KBX[:], True, True), ["BOH", "KBX"], ["KA"])
        act(T.KRS[:], T.KA[:, 0:128], ["KA"], ["KRS"])
        cp(T.LPI[:], pia, ["pia"], ["LPI"])
        act(T.KRP[:], T.KRS[:].indirect(T.LPI[:]), ["KRS", "LPI"], ["KRP"])
        sp, nq, mnn, cl, bm, dsb, alt, dd = pr
        am, ef, sa, m_, ds, kep, k0, nan = (T["VP%d" % (i // 4)][:, (i % 4) * 128:(i % 4) * 128 + 128] for i in range(8))
        tt(nq, T.NP1[:].indirect(T.LPI[:]), T.NP2[:], OP.not_equal, ["NP1", "NP2", "LPI"], ["nq"])
        tt(mnn, T.NP1[:].indirect(T.LPI[:]), T.NP2[:], OP.min, ["NP1", "NP2", "LPI"], ["mnn"])
        cp(sp, T.S1[:].indirect(T.LPI[:]), ["S1", "LPI"], ["sp"])
        ts(am, T.KRS[:], 128.0, OP.is_ge, ["KRS", "VP0", "VP1"], ["am"])
        tt(cl, nq, mnn, OP.mult, ["nq", "mnn"], ["cl"])
        tt(sa, sp, am, OP.mult, ["sp", "am"], ["sa"])
        tt(bm, T.KRP[:], T.C128[:], OP.is_equal, ["KRP", "C128"], ["bm"])
        tt(m_, T.S1[:], sa, OP.max, ["S1", "sa"], ["m"])
        tt(ef, am, bm, OP.max, ["am", "bm"], ["ef"])
        tt(ds, T.SDV[:], m_, OP.subtract, ["SDV", "m"], ["ds"])
        tt(T.CLE[:], cl, ef, OP.mult, ["cl", "ef"], ["CLE"])
        op("t", lambda: mm(T.KA[:, 128:256], T.BOB[:], T.CLE[:], True, True), ["BOB", "CLE"], ["KA"])
        tt(dsb, ds, bm, OP.mult, ["ds", "bm"], ["dsb"])
        ts(kep, T.CLE[:], 0.0, OP.is_equal, ["CLE"], ["kep"])
        tt(alt, m_, dsb, OP.add, ["m", "dsb"], ["alt"])
        tt(k0, T.S1[:], kep, OP.mult, ["S1", "kep"], ["k0"])
        ts(k0, k0, 767.0, OP.max, ["k0"], ["k0"])
        ts(nan, T.KA[:, 128:256], 0.0, OP.is_equal, ["KA"], ["nan"])
        tt(dd, alt, k0, OP.subtract, ["alt", "k0"], ["dd"])
        tt(dsb, dd, nan, OP.mult, ["dd", "nan"], ["dsb"])
        tt(T.S2[:], k0, dsb, OP.add, ["k0", "dsb", "VP0", "VP1"], ["S2"])
        if t < NR - 1:
            ts(T.L0T[:], T.S2[:], 1023, AND, ["S2"], ["L0T"])
            ts(T.LE[:], T.L0T[:], C["QB"], OP.add, ["L0T", "cQB"], ["LE"])
    ts(T.L0T[:], T.S2[:], 10, SHR, ["S2"], ["L0T"])
    ts(T.YO[:], T.L0T[:], -1.0, OP.add, ["L0T"], ["YO"])
    dma("y", T.yp[:], T.YO[:], ["YO"], ["yp"])

    need = {"v": cnt["v"], "s": cnt["s"], "t": cnt["t"], "gp": cnt["g"], "ls": ls[0], "nm": 7, "hn": 7, "ft": 7, "fs": 7}
    for i in range(ndma[0]):
        need["d%d" % i] = 16
    for q in range(NR):
        if q != rank:
            need["ta%d" % q] = 8
            need["tb%d" % q] = ntb[q]
    wait("y", need)
